import numpy as np
import ml_dtypes


def mxq(x, axis, fmt="e4m3"):
    dtype, down = {"e4m3": (ml_dtypes.float8_e4m3fn, 7), "e5m2": (ml_dtypes.float8_e5m2, 14)}[fmt]
    v = np.moveaxis(np.asarray(x, np.float32).astype(ml_dtypes.bfloat16).astype(np.float64), axis, -1)
    blocks = v.reshape(v.shape[:-1] + (-1, 32))
    amax = np.abs(blocks).max(-1, keepdims=True)
    byte = np.maximum(np.where(amax > 0, np.frexp(amax)[1] - 1 + 127, 0) - down, 1)
    scale = np.exp2(byte - 127.0)
    codes = (blocks / scale).astype(np.float32).astype(dtype).astype(np.float64)
    return np.moveaxis((codes * scale).reshape(v.shape), -1, axis)


WIDE = False


def mx_kscale(k):
    if not WIDE:
        return np.ones(k)
    levels = np.array([10, -10, 5, -5, 0])
    if k % 512:
        return np.exp2(np.random.permutation(np.resize(levels, k // 32))).repeat(32)
    a = np.empty((k // 512, 16))
    for p in range(k // 512):
        a[p, :8] = np.random.permutation(np.resize(levels, 8))
        for g in range(8):
            far = levels[np.abs(levels - a[p, g]) >= 10]
            a[p, g + 8] = far[np.random.randint(len(far))]
    return np.exp2(a.ravel()).repeat(32)


def f64(x):
    return np.asarray(x).astype(np.float64)


def striped(idx):
    return np.tile(idx.reshape(-1, 16).T, (8, 1)).astype(np.uint16)


def unstriped(offs):
    return offs[:16].T.reshape(-1).astype(np.int64)


def pack_weight(w):
    k, n = w.shape
    w = f64(np.asarray(w, np.float32).astype(ml_dtypes.bfloat16)).reshape(k // 32, 32, n)
    amax = np.abs(w).max(1)
    byte = np.clip(np.where(amax > 0, np.frexp(amax)[1] - 1 + 127 - 7, 1), 1, 254)
    scaled = (w * np.exp2(127.0 - byte)[:, None, :]).reshape(k, n).astype(np.float32)
    words = np.ascontiguousarray(scaled.reshape(k // 512, 128, 4, n).transpose(0, 1, 3, 2)).astype(ml_dtypes.float8_e4m3fn).view(np.uint8)
    return words, np.ascontiguousarray(byte.astype(np.uint8).reshape(k // 512, 16, n))


def unpack_weight(words, scales):
    g, p, n, _ = words.shape
    vals = np.ascontiguousarray(words).view(ml_dtypes.float8_e4m3fn).astype(np.float64) * np.repeat(np.exp2(scales.astype(np.float64) - 127.0), 8, axis=1)[..., None]
    return vals.transpose(0, 1, 3, 2).reshape(g * 512, n)


def sigmoid(v):
    return 1.0 / (1.0 + np.exp(-np.maximum(v, -700.0)))

def planes(y):
    n, m = y.shape
    v = y.astype(np.float32).astype(ml_dtypes.bfloat16).astype(np.float64).reshape(n // 32, 32, m)
    top = np.abs(v).max(1)
    byte = np.clip(np.where(top > 0, np.frexp(top)[1] - 1 + 127 - 7, 1), 1, 254)
    codes = (v * np.exp2(127.0 - byte)[:, None, :]).reshape(n, m).astype(np.float32).astype(ml_dtypes.float8_e4m3fn).view(np.uint8)
    words = codes.reshape(n // 512, 128, 4, m).transpose(0, 1, 3, 2)
    return np.ascontiguousarray(words), np.ascontiguousarray(byte.astype(np.uint8).reshape(n // 512, 16, m))


K, T, S, N, U = 512, 1024, 512, 512, 1024


def setup_inputs():
    n = np.random.standard_normal
    s = mx_kscale(K)[:, None]
    packed_xT = pack_weight(n((K, T)) * s)
    return {
        "x_words": packed_xT[0],
        "x_scales": packed_xT[1],
        "mem": n((N, U)).astype(np.float32),
        "w1": (n((K, N)) / np.sqrt(K) / s).astype(np.float32),
        "w2": (n((K, N)) / np.sqrt(K) / s).astype(np.float32),
        "offs": striped(np.random.permutation(T)[:S]),
        "slot": striped(np.random.permutation(U)[:S]),
    }


def reference(x_words, x_scales, mem, w1, w2, offs, slot):
    old = f64(mem)[:, unstriped(slot)]
    xq = unpack_weight(x_words, x_scales)[:, unstriped(offs)]
    g = sigmoid(mxq(f64(w2), 0, "e4m3").T @ xq)
    y = np.tanh(mxq(f64(w1), 0, "e4m3").T @ xq)
    out = f64(mem).copy()
    out[:, unstriped(slot)] = old + g * (y - old)
    return (out,) + planes(out)

@@ -1,0 +1,116 @@
+from contextlib import ExitStack
+
+import concourse.mybir as mybir
+
+K, T, S, N, U = 512, 1024, 512, 512, 1024
+FLOPS = 2 * 2 * K * N * S
+
+F32 = mybir.dt.float32
+BF16 = mybir.dt.bfloat16
+I32 = mybir.dt.int32
+U32 = mybir.dt.uint32
+U16 = mybir.dt.uint16
+U8 = mybir.dt.uint8
+FP8X4 = mybir.dt.float8_e4m3fn_x4
+ACT = mybir.ActivationFunctionType
+ALU = mybir.AluOpType
+
+P = 128
+PACK = 4
+ORDER = (0, 2, 3, 1)
+VEC_M = 42
+TAIL = 256
+
+
+def tile_picked_gmem_tanh_po_kernel(tc, x_words, x_scales, mem, w1, w2, offs, slot, out_0, out_1, out_2):
+    nc = tc.nc
+    with ExitStack() as ctx:
+        keep = ctx.enter_context(tc.tile_pool(name="keep", bufs=1))
+        psum = ctx.enter_context(tc.psum_pool(name="psum", bufs=1))
+
+        offs_t = keep.tile([P, S // 16], U16, name="offs_t")
+        slot_t = keep.tile([P, S // 16], U16, name="slot_t")
+        xw = keep.tile([P, T], I32, name="xw", align_bytes=64)
+        xs = keep.tile([P, T], U8, name="xs", align_bytes=64)
+        nc.vector.memset(xs[:].bitcast(I32), 0)
+        nc.sync.dma_start(offs_t[:], offs)
+        nc.sync.dma_start(xw[:], x_words[0].rearrange("p c r -> p (c r)").bitcast(I32))
+        nc.sync.dma_start(slot_t[:], slot)
+        for q in range(4):
+            nc.scalar.dma_start(xs[32 * q : 32 * q + 4, :].bitcast(I32), x_scales[0, 4 * q : 4 * q + 4, :].bitcast(I32))
+        raws = {}
+        for i, w in enumerate((w2, w1)):
+            for h in range(2):
+                raws[i, h] = keep.tile([P, PACK, N // 2], F32, name="raw%d_%d" % (i, h))
+                nc.sync.dma_start(raws[i, h][:], w.rearrange("(p j) m -> p j m", j=PACK)[:, :, h * 256 : (h + 1) * 256])
+        mem_rows = mem.rearrange("(p t) u -> p t u", t=PACK)
+        out_rows = out_0.rearrange("(p t) u -> p t u", t=PACK)
+        win = {}
+        for t in ORDER:
+            win[t] = keep.tile([P, U], F32, name="win%d" % t, tag="win%d" % t)
+            nc.sync.dma_start(win[t][:], mem_rows[:, t, :])
+
+        xs_g = keep.tile([P, S], U8, name="xs_g", align_bytes=64)
+        xw_g = keep.tile([P, S], U32, name="xw_g", align_bytes=64)
+        nc.vector.tensor_copy(xs_g[:], xs[:].indirect(offs_t[:]))
+        nc.vector.tensor_copy(xw_g[:], xw[:].bitcast(U32).indirect(offs_t[:]))
+
+        acc = {}
+        for i in range(2):
+            grouped = keep.tile([P, PACK, P, PACK], BF16, name="grp%d" % i, align_bytes=64)
+            for h in range(2):
+                dst = grouped[:, :, 64 * h : 64 * h + 64, :].rearrange("p t m j -> p m t j")
+                src = raws[i, h][:].rearrange("p j (m t) -> p m t j", t=PACK)
+                if (i, h) == (1, 1):
+                    nc.vector.tensor_copy(dst[:, :VEC_M], src[:, :VEC_M])
+                    nc.scalar.copy(dst[:, VEC_M:], src[:, VEC_M:])
+                elif h == 0:
+                    nc.scalar.copy(dst, src)
+                else:
+                    nc.vector.tensor_copy(dst, src)
+            codes = keep.tile([P, N], U32, name="codes%d" % i, align_bytes=64)
+            scales = keep.tile([P, N], U8, name="scales%d" % i, align_bytes=64)
+            flat = grouped[:].rearrange("p t m j -> p (t m j)")
+            for t0, t1 in ((0, 1), (2, 4), (1, 2)):
+                cols = slice(t0 * P, t1 * P)
+                nc.vector.quantize_mx(codes[:, cols].bitcast(FP8X4), scales[:, cols], flat[:, t0 * 512 : t1 * 512])
+            for t in ORDER:
+                cols = slice(t * P, (t + 1) * P)
+                acc[i, t] = psum.tile([P, S], F32, name="acc%d_%d" % (i, t))
+                nc.tensor.matmul_mx(acc[i, t][:], lhsT=codes[:, cols].bitcast(FP8X4), lhsT_scale=scales[:, cols],
+                                    rhs=xw_g[:].bitcast(FP8X4), rhs_scale=xs_g[:], start=True, stop=True)
+        act = {}
+        for t in ORDER:
+            for i, func in enumerate((ACT.Sigmoid, ACT.Tanh)):
+                act[i, t] = keep.tile([P, S], F32, name="act%d_%d" % (i, t))
+                nc.scalar.activation(act[i, t][:], acc[i, t][:], func, scale=-1.0)
+
+        rounded = keep.tile([P, U, PACK], BF16, name="rounded", align_bytes=64)
+        o_codes = keep.tile([P, U], I32, name="o_codes", align_bytes=64)
+        o_scales = keep.tile([P, U], U8, name="o_scales", align_bytes=64)
+        for t in ORDER:
+            tag = "win%d" % ORDER[0] if t == ORDER[-1] else "kept%d" % t
+            kept = keep.tile([P, S], F32, name="kept%d" % t, tag=tag)
+            nc.vector.tensor_tensor(kept[:], win[t][:].indirect(slot_t[:]), act[0, t][:], ALU.mult)
+            fresh = keep.tile([P, S], F32, name="fresh%d" % t)
+            nc.vector.scalar_tensor_tensor(fresh[:], act[0, t][:], 1.0, act[1, t][:], ALU.subtract, ALU.mult)
+            nc.vector.tensor_tensor(win[t][:].indirect(slot_t[:]), kept[:], fresh[:], ALU.add)
+            nc.sync.dma_start(out_rows[:, t, :], win[t][:])
+            if t != ORDER[-1]:
+                nc.scalar.copy(rounded[:, :, t], win[t][:])
+        t = ORDER[-1]
+        flat = rounded[:].rearrange("p u t -> p (u t)")
+        words_out = out_1[0].rearrange("p c r -> p (c r)").bitcast(I32)
+        for c in (0, 2, 1, 3):
+            cols = slice(c * TAIL, (c + 1) * TAIL)
+            if c < 2:
+                nc.vector.tensor_copy(rounded[:, cols, t], win[t][:, cols])
+            else:
+                nc.scalar.copy(rounded[:, cols, t], win[t][:, cols])
+        for c in range(4):
+            cols = slice(c * TAIL, (c + 1) * TAIL)
+            nc.vector.quantize_mx(o_codes[:, cols].bitcast(FP8X4), o_scales[:, cols], flat[:, c * TAIL * 4 : (c + 1) * TAIL * 4])
+            nc.sync.dma_start(words_out[:, cols], o_codes[:, cols])
+        for q in range(4):
+            eng = nc.scalar if q % 2 else nc.sync
+            eng.dma_start(out_2[0, 4 * q : 4 * q + 4, :].bitcast(I32), o_scales[32 * q : 32 * q + 4, :].bitcast(I32))

@@ -33,16 +33,22 @@ def tile_picked_gmem_tanh_po_kernel(tc, x_words, x_scales, mem, w1, w2, offs, sl
         xw = keep.tile([P, T], I32, name="xw", align_bytes=64)
         xs = keep.tile([P, T], U8, name="xs", align_bytes=64)
         nc.vector.memset(xs[:].bitcast(I32), 0)
+        warm = keep.tile([P, 2], F32, name="warm")
+        nc.vector.memset(warm[:, 0:1], 0.0)
         nc.sync.dma_start(offs_t[:], offs)
         nc.sync.dma_start(xw[:], x_words[0].rearrange("p c r -> p (c r)").bitcast(I32))
         nc.sync.dma_start(slot_t[:], slot)
         for q in range(4):
-            nc.scalar.dma_start(xs[32 * q : 32 * q + 4, :].bitcast(I32), x_scales[0, 4 * q : 4 * q + 4, :].bitcast(I32))
+            nc.sync.dma_start(xs[32 * q : 32 * q + 4, :].bitcast(I32), x_scales[0, 4 * q : 4 * q + 4, :].bitcast(I32))
+        nc.scalar.activation(warm[:, 1:2], warm[:, 0:1], ACT.Sigmoid)
         raws = {}
-        for i, w in enumerate((w2, w1)):
-            for h in range(2):
-                raws[i, h] = keep.tile([P, PACK, N // 2], F32, name="raw%d_%d" % (i, h))
-                nc.sync.dma_start(raws[i, h][:], w.rearrange("(p j) m -> p j m", j=PACK)[:, :, h * 256 : (h + 1) * 256])
+        raw2 = keep.tile([P, PACK, N], F32, name="raw2")
+        nc.sync.dma_start(raw2[:], w2.rearrange("(p j) m -> p j m", j=PACK))
+        for h in range(2):
+            raws[0, h] = raw2[:, :, h * 256 : (h + 1) * 256]
+            raw1 = keep.tile([P, PACK, N // 2], F32, name="raw1_%d" % h)
+            nc.sync.dma_start(raw1[:], w1.rearrange("(p j) m -> p j m", j=PACK)[:, :, h * 256 : (h + 1) * 256])
+            raws[1, h] = raw1[:]
         mem_rows = mem.rearrange("(p t) u -> p t u", t=PACK)
         out_rows = out_0.rearrange("(p t) u -> p t u", t=PACK)
         win = {}
@@ -60,11 +66,8 @@ def tile_picked_gmem_tanh_po_kernel(tc, x_words, x_scales, mem, w1, w2, offs, sl
             grouped = keep.tile([P, PACK, P, PACK], BF16, name="grp%d" % i, align_bytes=64)
             for h in range(2):
                 dst = grouped[:, :, 64 * h : 64 * h + 64, :].rearrange("p t m j -> p m t j")
-                src = raws[i, h][:].rearrange("p j (m t) -> p m t j", t=PACK)
-                if (i, h) == (1, 1):
-                    nc.vector.tensor_copy(dst[:, :VEC_M], src[:, :VEC_M])
-                    nc.scalar.copy(dst[:, VEC_M:], src[:, VEC_M:])
-                elif h == 0:
+                src = raws[i, h].rearrange("p j (m t) -> p m t j", t=PACK)
+                if h == 0:
                     nc.scalar.copy(dst, src)
                 else:
                     nc.vector.tensor_copy(dst, src)
@@ -74,16 +77,17 @@ def tile_picked_gmem_tanh_po_kernel(tc, x_words, x_scales, mem, w1, w2, offs, sl
             for t0, t1 in ((0, 1), (2, 4), (1, 2)):
                 cols = slice(t0 * P, t1 * P)
                 nc.vector.quantize_mx(codes[:, cols].bitcast(FP8X4), scales[:, cols], flat[:, t0 * 512 : t1 * 512])
-            for t in ORDER:
-                cols = slice(t * P, (t + 1) * P)
-                acc[i, t] = psum.tile([P, S], F32, name="acc%d_%d" % (i, t))
-                nc.tensor.matmul_mx(acc[i, t][:], lhsT=codes[:, cols].bitcast(FP8X4), lhsT_scale=scales[:, cols],
-                                    rhs=xw_g[:].bitcast(FP8X4), rhs_scale=xs_g[:], start=True, stop=True)
+            acc[i] = (codes, scales)
         act = {}
-        for t in ORDER:
+        for n, t in enumerate(ORDER):
+            cols = slice(t * P, (t + 1) * P)
             for i, func in enumerate((ACT.Sigmoid, ACT.Tanh)):
+                codes, scales = acc[i]
+                bank = psum.tile([P, S], F32, name="bank%d_%d" % (i, t), tag="bank%d" % (n + i))
+                nc.tensor.matmul_mx(bank[:], lhsT=codes[:, cols].bitcast(FP8X4), lhsT_scale=scales[:, cols],
+                                    rhs=xw_g[:].bitcast(FP8X4), rhs_scale=xs_g[:], start=True, stop=True)
                 act[i, t] = keep.tile([P, S], F32, name="act%d_%d" % (i, t))
-                nc.scalar.activation(act[i, t][:], acc[i, t][:], func, scale=-1.0)
+                nc.scalar.activation(act[i, t][:], bank[:], func, scale=-1.0)
 
         rounded = keep.tile([P, U, PACK], BF16, name="rounded", align_bytes=64)
         o_codes = keep.tile([P, U], I32, name="o_codes", align_bytes=64)

@@ -18,7 +18,6 @@ ALU = mybir.AluOpType
 P = 128
 PACK = 4
 ORDER = (0, 2, 3, 1)
-VEC_M = 42
 TAIL = 256
 
 
@@ -35,20 +34,18 @@ def tile_picked_gmem_tanh_po_kernel(tc, x_words, x_scales, mem, w1, w2, offs, sl
         nc.vector.memset(xs[:].bitcast(I32), 0)
         warm = keep.tile([P, 2], F32, name="warm")
         nc.vector.memset(warm[:, 0:1], 0.0)
-        nc.sync.dma_start(offs_t[:], offs)
         nc.sync.dma_start(xw[:], x_words[0].rearrange("p c r -> p (c r)").bitcast(I32))
+        nc.sync.dma_start(offs_t[:], offs)
         nc.sync.dma_start(slot_t[:], slot)
         for q in range(4):
             nc.sync.dma_start(xs[32 * q : 32 * q + 4, :].bitcast(I32), x_scales[0, 4 * q : 4 * q + 4, :].bitcast(I32))
         nc.scalar.activation(warm[:, 1:2], warm[:, 0:1], ACT.Sigmoid)
-        raws = {}
         raw2 = keep.tile([P, PACK, N], F32, name="raw2")
         nc.sync.dma_start(raw2[:], w2.rearrange("(p j) m -> p j m", j=PACK))
+        raw1 = {}
         for h in range(2):
-            raws[0, h] = raw2[:, :, h * 256 : (h + 1) * 256]
-            raw1 = keep.tile([P, PACK, N // 2], F32, name="raw1_%d" % h)
-            nc.sync.dma_start(raw1[:], w1.rearrange("(p j) m -> p j m", j=PACK)[:, :, h * 256 : (h + 1) * 256])
-            raws[1, h] = raw1[:]
+            raw1[h] = keep.tile([P, 2, N], F32, name="raw1_%d" % h, tag="raw1_%d" % h)
+            nc.sync.dma_start(raw1[h][:], w1.rearrange("(p j) m -> p j m", j=PACK)[:, 2 * h : 2 * h + 2, :])
         mem_rows = mem.rearrange("(p t) u -> p t u", t=PACK)
         out_rows = out_0.rearrange("(p t) u -> p t u", t=PACK)
         win = {}
@@ -58,50 +55,75 @@ def tile_picked_gmem_tanh_po_kernel(tc, x_words, x_scales, mem, w1, w2, offs, sl
 
         xs_g = keep.tile([P, S], U8, name="xs_g", align_bytes=64)
         xw_g = keep.tile([P, S], U32, name="xw_g", align_bytes=64)
-        nc.vector.tensor_copy(xs_g[:], xs[:].indirect(offs_t[:]))
         nc.vector.tensor_copy(xw_g[:], xw[:].bitcast(U32).indirect(offs_t[:]))
+        nc.vector.tensor_copy(xs_g[:], xs[:].indirect(offs_t[:]))
 
-        acc = {}
-        for i in range(2):
-            grouped = keep.tile([P, PACK, P, PACK], BF16, name="grp%d" % i, align_bytes=64)
-            for h in range(2):
-                dst = grouped[:, :, 64 * h : 64 * h + 64, :].rearrange("p t m j -> p m t j")
-                src = raws[i, h].rearrange("p j (m t) -> p m t j", t=PACK)
-                if h == 0:
-                    nc.scalar.copy(dst, src)
-                else:
-                    nc.vector.tensor_copy(dst, src)
-            codes = keep.tile([P, N], U32, name="codes%d" % i, align_bytes=64)
-            scales = keep.tile([P, N], U8, name="scales%d" % i, align_bytes=64)
-            flat = grouped[:].rearrange("p t m j -> p (t m j)")
-            for t0, t1 in ((0, 1), (2, 4), (1, 2)):
-                cols = slice(t0 * P, t1 * P)
-                nc.vector.quantize_mx(codes[:, cols].bitcast(FP8X4), scales[:, cols], flat[:, t0 * 512 : t1 * 512])
-            acc[i] = (codes, scales)
+        def round_rows(grouped, raw, j0, j1, cut):
+            dst = grouped[:, :, :, j0:j1].rearrange("p t m j -> p m j t")
+            src = raw.rearrange("p j (m t) -> p m j t", t=PACK)
+            nc.scalar.copy(dst[:, :cut], src[:, :cut])
+            nc.vector.tensor_copy(dst[:, cut:], src[:, cut:])
+
+        def quantise(grouped, name):
+            codes = keep.tile([P, N], U32, name="codes" + name, align_bytes=64)
+            scales = keep.tile([P, N], U8, name="scales" + name, align_bytes=64)
+            nc.vector.quantize_mx(codes[:].bitcast(FP8X4), scales[:], grouped[:].rearrange("p t m j -> p (t m j)"))
+            return codes, scales
+
+        grouped2 = keep.tile([P, PACK, P, PACK], BF16, name="grouped2", align_bytes=64)
+        round_rows(grouped2, raw2[:], 0, 4, 44)
+        acc = {0: quantise(grouped2, "2")}
+        grouped1 = keep.tile([P, PACK, P, PACK], BF16, name="grouped1", align_bytes=64)
+        round_rows(grouped1, raw1[0][:], 0, 2, 80)
+        round_rows(grouped1, raw1[1][:], 2, 4, 44)
+        acc[1] = quantise(grouped1, "1")
+
         act = {}
-        for n, t in enumerate(ORDER):
+        gates = keep.tile([P, PACK, S], F32, name="gates", tag="raw1_1")
+        cands = keep.tile([P, PACK, S], F32, name="cands")
+        for i, n in ((0,0), (0,1), (1,0), (1,1), (0,2), (1,2), (0,3), (1,3)):
+            t = ORDER[n]
             cols = slice(t * P, (t + 1) * P)
-            for i, func in enumerate((ACT.Sigmoid, ACT.Tanh)):
-                codes, scales = acc[i]
-                bank = psum.tile([P, S], F32, name="bank%d_%d" % (i, t), tag="bank%d" % (n + i))
-                nc.tensor.matmul_mx(bank[:], lhsT=codes[:, cols].bitcast(FP8X4), lhsT_scale=scales[:, cols],
-                                    rhs=xw_g[:].bitcast(FP8X4), rhs_scale=xs_g[:], start=True, stop=True)
-                act[i, t] = keep.tile([P, S], F32, name="act%d_%d" % (i, t))
-                nc.scalar.activation(act[i, t][:], bank[:], func, scale=-1.0)
+            codes, scales = acc[i]
+            bank = psum.tile([P, S], F32, name="bank%d_%d" % (i, t))
+            nc.tensor.matmul_mx(bank[:], lhsT=codes[:, cols].bitcast(FP8X4), lhsT_scale=scales[:, cols],
+                                rhs=xw_g[:].bitcast(FP8X4), rhs_scale=xs_g[:], start=True, stop=True)
+            act[i, t] = (gates, cands)[i][:, n, :]
+            nc.scalar.activation(act[i, t], bank[:], (ACT.Sigmoid, ACT.Tanh)[i], scale=-1.0)
 
         rounded = keep.tile([P, U, PACK], BF16, name="rounded", align_bytes=64)
         o_codes = keep.tile([P, U], I32, name="o_codes", align_bytes=64)
         o_scales = keep.tile([P, U], U8, name="o_scales", align_bytes=64)
-        for t in ORDER:
-            tag = "win%d" % ORDER[0] if t == ORDER[-1] else "kept%d" % t
-            kept = keep.tile([P, S], F32, name="kept%d" % t, tag=tag)
-            nc.vector.tensor_tensor(kept[:], win[t][:].indirect(slot_t[:]), act[0, t][:], ALU.mult)
-            fresh = keep.tile([P, S], F32, name="fresh%d" % t)
-            nc.vector.scalar_tensor_tensor(fresh[:], act[0, t][:], 1.0, act[1, t][:], ALU.subtract, ALU.mult)
-            nc.vector.tensor_tensor(win[t][:].indirect(slot_t[:]), kept[:], fresh[:], ALU.add)
+        kept, fresh = {}, {}
+
+        def look_up(t, dst):
+            kept[t] = dst
+            nc.vector.tensor_tensor(dst, win[t][:].indirect(slot_t[:]), act[0, t], ALU.mult)
+
+        def blend(t):
+            fresh[t] = keep.tile([P, S], F32, name="fresh%d" % t)
+            nc.vector.scalar_tensor_tensor(fresh[t][:], act[0, t], 1.0, act[1, t], ALU.subtract, ALU.mult)
+
+        def put(t):
+            nc.vector.tensor_tensor(win[t][:].indirect(slot_t[:]), kept[t], fresh[t][:], ALU.add)
             nc.sync.dma_start(out_rows[:, t, :], win[t][:])
             if t != ORDER[-1]:
                 nc.scalar.copy(rounded[:, :, t], win[t][:])
+
+        early = keep.tile([P, 2, S], F32, name="early")
+        look_up(ORDER[0], early[:, 0, :])
+        look_up(ORDER[1], early[:, 1, :])
+        blend(ORDER[0])
+        blend(ORDER[1])
+        put(ORDER[0])
+        blend(ORDER[2])
+        blend(ORDER[3])
+        put(ORDER[1])
+        late = keep.tile([P, 2, S], F32, name="late", tag="win%d" % ORDER[0])
+        look_up(ORDER[2], late[:, 0, :])
+        look_up(ORDER[3], late[:, 1, :])
+        put(ORDER[2])
+        put(ORDER[3])
         t = ORDER[-1]
         flat = rounded[:].rearrange("p u t -> p (u t)")
         words_out = out_1[0].rearrange("p c r -> p (c r)").bitcast(I32)
@@ -114,7 +136,9 @@ def tile_picked_gmem_tanh_po_kernel(tc, x_words, x_scales, mem, w1, w2, offs, sl
         for c in range(4):
             cols = slice(c * TAIL, (c + 1) * TAIL)
             nc.vector.quantize_mx(o_codes[:, cols].bitcast(FP8X4), o_scales[:, cols], flat[:, c * TAIL * 4 : (c + 1) * TAIL * 4])
-            nc.sync.dma_start(words_out[:, cols], o_codes[:, cols])
+            if c > 0:
+                done = slice(0 if c == 1 else c * TAIL, (c + 1) * TAIL)
+                nc.sync.dma_start(words_out[:, done], o_codes[:, done])
         for q in range(4):
             eng = nc.scalar if q % 2 else nc.sync
             eng.dma_start(out_2[0, 4 * q : 4 * q + 4, :].bitcast(I32), o_scales[32 * q : 32 * q + 4, :].bitcast(I32))

@@ -42,10 +42,8 @@ def tile_picked_gmem_tanh_po_kernel(tc, x_words, x_scales, mem, w1, w2, offs, sl
         nc.scalar.activation(warm[:, 1:2], warm[:, 0:1], ACT.Sigmoid)
         raw2 = keep.tile([P, PACK, N], F32, name="raw2")
         nc.sync.dma_start(raw2[:], w2.rearrange("(p j) m -> p j m", j=PACK))
-        raw1 = {}
-        for h in range(2):
-            raw1[h] = keep.tile([P, 2, N], F32, name="raw1_%d" % h, tag="raw1_%d" % h)
-            nc.sync.dma_start(raw1[h][:], w1.rearrange("(p j) m -> p j m", j=PACK)[:, 2 * h : 2 * h + 2, :])
+        raw1 = keep.tile([P, PACK, N], F32, name="raw1", tag="raw1")
+        nc.sync.dma_start(raw1[:], w1.rearrange("(p j) m -> p j m", j=PACK))
         mem_rows = mem.rearrange("(p t) u -> p t u", t=PACK)
         out_rows = out_0.rearrange("(p t) u -> p t u", t=PACK)
         win = {}
@@ -58,28 +56,31 @@ def tile_picked_gmem_tanh_po_kernel(tc, x_words, x_scales, mem, w1, w2, offs, sl
         nc.vector.tensor_copy(xw_g[:], xw[:].bitcast(U32).indirect(offs_t[:]))
         nc.vector.tensor_copy(xs_g[:], xs[:].indirect(offs_t[:]))
 
-        def round_rows(grouped, raw, j0, j1, cut):
-            dst = grouped[:, :, :, j0:j1].rearrange("p t m j -> p m j t")
-            src = raw.rearrange("p j (m t) -> p m j t", t=PACK)
-            nc.scalar.copy(dst[:, :cut], src[:, :cut])
-            nc.vector.tensor_copy(dst[:, cut:], src[:, cut:])
-
-        def quantise(grouped, name):
+        def quantise(raw, name, on_scalar, on_vector, runs):
+            grouped = keep.tile([P, PACK, P, PACK], BF16, name="grouped" + name, align_bytes=64)
+            dst = grouped[:].rearrange("p t m j -> p m j t")
+            src = raw[:].rearrange("p j (m t) -> p m j t", t=PACK)
+            for ms, ts in on_scalar:
+                nc.scalar.copy(dst[:, ms, :, ts], src[:, ms, :, ts])
+            for ms, ts in on_vector:
+                nc.vector.tensor_copy(dst[:, ms, :, ts], src[:, ms, :, ts])
             codes = keep.tile([P, N], U32, name="codes" + name, align_bytes=64)
             scales = keep.tile([P, N], U8, name="scales" + name, align_bytes=64)
-            nc.vector.quantize_mx(codes[:].bitcast(FP8X4), scales[:], grouped[:].rearrange("p t m j -> p (t m j)"))
+            flat = grouped[:].rearrange("p t m j -> p (t m j)")
+            for t0, t1 in runs:
+                cols = slice(t0 * P, t1 * P)
+                nc.vector.quantize_mx(codes[:, cols].bitcast(FP8X4), scales[:, cols], flat[:, t0 * 512 : t1 * 512])
             return codes, scales
 
-        grouped2 = keep.tile([P, PACK, P, PACK], BF16, name="grouped2", align_bytes=64)
-        round_rows(grouped2, raw2[:], 0, 4, 44)
-        acc = {0: quantise(grouped2, "2")}
-        grouped1 = keep.tile([P, PACK, P, PACK], BF16, name="grouped1", align_bytes=64)
-        round_rows(grouped1, raw1[0][:], 0, 2, 80)
-        round_rows(grouped1, raw1[1][:], 2, 4, 44)
-        acc[1] = quantise(grouped1, "1")
+        low, high, every = slice(0, 2), slice(2, 4), slice(0, P)
+        acc = {
+            0: quantise(raw2, "2", ((slice(0, 40), low), (slice(0, 64), high)), ((slice(40, P), low), (slice(64, P), high)), ((0, 1), (1, 2), (2, 4))),
+            1: quantise(raw1, "1", ((slice(0, 72), high),), ((every, low), (slice(72, P), high)), ((0, 2), (2, 4))),
+        }
 
         act = {}
-        gates = keep.tile([P, PACK, S], F32, name="gates", tag="raw1_1")
+        gate0 = keep.tile([P, S], F32, name="gate0")
+        gates = keep.tile([P, PACK - 1, S], F32, name="gates", tag="raw1")
         cands = keep.tile([P, PACK, S], F32, name="cands")
         for i, n in ((0,0), (0,1), (1,0), (1,1), (0,2), (1,2), (0,3), (1,3)):
             t = ORDER[n]
@@ -88,7 +89,7 @@ def tile_picked_gmem_tanh_po_kernel(tc, x_words, x_scales, mem, w1, w2, offs, sl
             bank = psum.tile([P, S], F32, name="bank%d_%d" % (i, t))
             nc.tensor.matmul_mx(bank[:], lhsT=codes[:, cols].bitcast(FP8X4), lhsT_scale=scales[:, cols],
                                 rhs=xw_g[:].bitcast(FP8X4), rhs_scale=xs_g[:], start=True, stop=True)
-            act[i, t] = (gates, cands)[i][:, n, :]
+            act[i, t] = cands[:, n, :] if i else (gates[:, n - 1, :] if n else gate0[:])
             nc.scalar.activation(act[i, t], bank[:], (ACT.Sigmoid, ACT.Tanh)[i], scale=-1.0)
 
         rounded = keep.tile([P, U, PACK], BF16, name="rounded", align_bytes=64)
@@ -110,9 +111,10 @@ def tile_picked_gmem_tanh_po_kernel(tc, x_words, x_scales, mem, w1, w2, offs, sl
             if t != ORDER[-1]:
                 nc.scalar.copy(rounded[:, :, t], win[t][:])
 
-        early = keep.tile([P, 2, S], F32, name="early")
-        look_up(ORDER[0], early[:, 0, :])
-        look_up(ORDER[1], early[:, 1, :])
+        early = keep.tile([P, S], F32, name="early")
+        early1 = keep.tile([P, S], F32, name="early1")
+        look_up(ORDER[0], early[:])
+        look_up(ORDER[1], early1[:])
         blend(ORDER[0])
         blend(ORDER[1])
         put(ORDER[0])

@@ -81,16 +81,24 @@ def tile_picked_gmem_tanh_po_kernel(tc, x_words, x_scales, mem, w1, w2, offs, sl
         act = {}
         gate0 = keep.tile([P, S], F32, name="gate0")
         gates = keep.tile([P, PACK - 1, S], F32, name="gates", tag="raw1")
-        cands = keep.tile([P, PACK, S], F32, name="cands")
-        for i, n in ((0,0), (0,1), (1,0), (1,1), (0,2), (1,2), (0,3), (1,3)):
+        cands = keep.tile([P, 2, S], F32, name="cands")
+
+        def product(i, n, dst):
             t = ORDER[n]
             cols = slice(t * P, (t + 1) * P)
             codes, scales = acc[i]
-            bank = psum.tile([P, S], F32, name="bank%d_%d" % (i, t))
+            bank = psum.tile([P, S], F32, name="bank%d_%d" % (i, t), tag="bank%d" % (2 + n if i else n))
             nc.tensor.matmul_mx(bank[:], lhsT=codes[:, cols].bitcast(FP8X4), lhsT_scale=scales[:, cols],
                                 rhs=xw_g[:].bitcast(FP8X4), rhs_scale=xs_g[:], start=True, stop=True)
-            act[i, t] = cands[:, n, :] if i else (gates[:, n - 1, :] if n else gate0[:])
-            nc.scalar.activation(act[i, t], bank[:], (ACT.Sigmoid, ACT.Tanh)[i], scale=-1.0)
+            act[i, t] = dst
+            nc.scalar.activation(dst, bank[:], (ACT.Sigmoid, ACT.Tanh)[i], scale=-1.0)
+
+        product(0, 0, gate0[:])
+        product(0, 1, gates[:, 0, :])
+        product(1, 0, cands[:, 0, :])
+        product(1, 1, cands[:, 1, :])
+        product(0, 2, gates[:, 1, :])
+        product(0, 3, gates[:, 2, :])
 
         rounded = keep.tile([P, U, PACK], BF16, name="rounded", align_bytes=64)
         o_codes = keep.tile([P, U], I32, name="o_codes", align_bytes=64)
@@ -111,19 +119,22 @@ def tile_picked_gmem_tanh_po_kernel(tc, x_words, x_scales, mem, w1, w2, offs, sl
             if t != ORDER[-1]:
                 nc.scalar.copy(rounded[:, :, t], win[t][:])
 
-        early = keep.tile([P, S], F32, name="early")
-        early1 = keep.tile([P, S], F32, name="early1")
-        look_up(ORDER[0], early[:])
-        look_up(ORDER[1], early1[:])
+        for n in range(PACK):
+            kept[ORDER[n]] = keep.tile([P, S], F32, name="kept%d" % n, tag="kept%d" % n) if n else None
+        first = keep.tile([P, S], F32, name="first", tag="first")
+        look_up(ORDER[0], first[:])
+        look_up(ORDER[1], kept[ORDER[1]][:])
         blend(ORDER[0])
         blend(ORDER[1])
         put(ORDER[0])
+        late = keep.tile([P, 2, S], F32, name="late", tag="first")
+        product(1, 2, late[:, 0, :])
+        product(1, 3, late[:, 1, :])
+        look_up(ORDER[2], kept[ORDER[2]][:])
+        look_up(ORDER[3], kept[ORDER[3]][:])
+        put(ORDER[1])
         blend(ORDER[2])
         blend(ORDER[3])
-        put(ORDER[1])
-        late = keep.tile([P, 2, S], F32, name="late", tag="win%d" % ORDER[0])
-        look_up(ORDER[2], late[:, 0, :])
-        look_up(ORDER[3], late[:, 1, :])
         put(ORDER[2])
         put(ORDER[3])
         t = ORDER[-1]
@@ -138,9 +149,9 @@ def tile_picked_gmem_tanh_po_kernel(tc, x_words, x_scales, mem, w1, w2, offs, sl
         for c in range(4):
             cols = slice(c * TAIL, (c + 1) * TAIL)
             nc.vector.quantize_mx(o_codes[:, cols].bitcast(FP8X4), o_scales[:, cols], flat[:, c * TAIL * 4 : (c + 1) * TAIL * 4])
-            if c > 0:
-                done = slice(0 if c == 1 else c * TAIL, (c + 1) * TAIL)
+            if c != 1:
+                done = slice(TAIL if c == 2 else c * TAIL, (c + 1) * TAIL)
                 nc.sync.dma_start(words_out[:, done], o_codes[:, done])
         for q in range(4):
-            eng = nc.scalar if q % 2 else nc.sync
+            eng = nc.scalar if q else nc.sync
             eng.dma_start(out_2[0, 4 * q : 4 * q + 4, :].bitcast(I32), o_scales[32 * q : 32 * q + 4, :].bitcast(I32))

@@ -17,8 +17,17 @@ ALU = mybir.AluOpType
 
 P = 128
 PACK = 4
+QUADS = 4
+GATE, CAND = 0, 1
+
 ORDER = (0, 2, 3, 1)
-TAIL = 256
+
+LOW, HIGH = slice(0, 2), slice(2, 4)
+W2_LOW_CUT = 40
+W2_HIGH_CUT = 64
+W1_HIGH_CUT = 72
+
+CHUNK = 256
 
 
 def tile_picked_gmem_tanh_po_kernel(tc, x_words, x_scales, mem, w1, w2, offs, slot, out_0, out_1, out_2):
@@ -34,11 +43,13 @@ def tile_picked_gmem_tanh_po_kernel(tc, x_words, x_scales, mem, w1, w2, offs, sl
         nc.vector.memset(xs[:].bitcast(I32), 0)
         warm = keep.tile([P, 2], F32, name="warm")
         nc.vector.memset(warm[:, 0:1], 0.0)
+
         nc.sync.dma_start(xw[:], x_words[0].rearrange("p c r -> p (c r)").bitcast(I32))
         nc.sync.dma_start(offs_t[:], offs)
         nc.sync.dma_start(slot_t[:], slot)
-        for q in range(4):
-            nc.sync.dma_start(xs[32 * q : 32 * q + 4, :].bitcast(I32), x_scales[0, 4 * q : 4 * q + 4, :].bitcast(I32))
+        for q in range(QUADS):
+            queue = nc.scalar if q % 2 else nc.sync
+            queue.dma_start(xs[32 * q : 32 * q + 4, :].bitcast(I32), x_scales[0, 4 * q : 4 * q + 4, :].bitcast(I32))
         nc.scalar.activation(warm[:, 1:2], warm[:, 0:1], ACT.Sigmoid)
         raw2 = keep.tile([P, PACK, N], F32, name="raw2")
         nc.sync.dma_start(raw2[:], w2.rearrange("(p j) m -> p j m", j=PACK))
@@ -60,22 +71,31 @@ def tile_picked_gmem_tanh_po_kernel(tc, x_words, x_scales, mem, w1, w2, offs, sl
             grouped = keep.tile([P, PACK, P, PACK], BF16, name="grouped" + name, align_bytes=64)
             dst = grouped[:].rearrange("p t m j -> p m j t")
             src = raw[:].rearrange("p j (m t) -> p m j t", t=PACK)
-            for ms, ts in on_scalar:
-                nc.scalar.copy(dst[:, ms, :, ts], src[:, ms, :, ts])
-            for ms, ts in on_vector:
-                nc.vector.tensor_copy(dst[:, ms, :, ts], src[:, ms, :, ts])
+            for groups, phases in on_scalar:
+                nc.scalar.copy(dst[:, groups, :, phases], src[:, groups, :, phases])
+            for groups, phases in on_vector:
+                nc.vector.tensor_copy(dst[:, groups, :, phases], src[:, groups, :, phases])
             codes = keep.tile([P, N], U32, name="codes" + name, align_bytes=64)
             scales = keep.tile([P, N], U8, name="scales" + name, align_bytes=64)
-            flat = grouped[:].rearrange("p t m j -> p (t m j)")
+            values = grouped[:].rearrange("p t m j -> p (t m j)")
             for t0, t1 in runs:
                 cols = slice(t0 * P, t1 * P)
-                nc.vector.quantize_mx(codes[:, cols].bitcast(FP8X4), scales[:, cols], flat[:, t0 * 512 : t1 * 512])
+                nc.vector.quantize_mx(codes[:, cols].bitcast(FP8X4), scales[:, cols], values[:, t0 * P * PACK : t1 * P * PACK])
             return codes, scales
 
-        low, high, every = slice(0, 2), slice(2, 4), slice(0, P)
-        acc = {
-            0: quantise(raw2, "2", ((slice(0, 40), low), (slice(0, 64), high)), ((slice(40, P), low), (slice(64, P), high)), ((0, 1), (1, 2), (2, 4))),
-            1: quantise(raw1, "1", ((slice(0, 72), high),), ((every, low), (slice(72, P), high)), ((0, 2), (2, 4))),
+        weights = {
+            GATE: quantise(
+                raw2, "2",
+                ((slice(0, W2_LOW_CUT), LOW), (slice(0, W2_HIGH_CUT), HIGH)),
+                ((slice(W2_LOW_CUT, P), LOW), (slice(W2_HIGH_CUT, P), HIGH)),
+                ((0, 1), (1, 2), (2, 4)),
+            ),
+            CAND: quantise(
+                raw1, "1",
+                ((slice(0, W1_HIGH_CUT), HIGH),),
+                ((slice(0, P), LOW), (slice(W1_HIGH_CUT, P), HIGH)),
+                ((0, 2), (2, 4)),
+            ),
         }
 
         act = {}
@@ -83,75 +103,76 @@ def tile_picked_gmem_tanh_po_kernel(tc, x_words, x_scales, mem, w1, w2, offs, sl
         gates = keep.tile([P, PACK - 1, S], F32, name="gates", tag="raw1")
         cands = keep.tile([P, 2, S], F32, name="cands")
 
-        def product(i, n, dst):
+        def product(kind, n, dst):
             t = ORDER[n]
             cols = slice(t * P, (t + 1) * P)
-            codes, scales = acc[i]
-            bank = psum.tile([P, S], F32, name="bank%d_%d" % (i, t), tag="bank%d" % (2 + n if i else n))
+            codes, scales = weights[kind]
+            bank = psum.tile([P, S], F32, name="bank%d_%d" % (kind, t), tag="bank%d" % (n + 2 * kind))
             nc.tensor.matmul_mx(bank[:], lhsT=codes[:, cols].bitcast(FP8X4), lhsT_scale=scales[:, cols],
                                 rhs=xw_g[:].bitcast(FP8X4), rhs_scale=xs_g[:], start=True, stop=True)
-            act[i, t] = dst
-            nc.scalar.activation(dst, bank[:], (ACT.Sigmoid, ACT.Tanh)[i], scale=-1.0)
+            act[kind, t] = dst
+            nc.scalar.activation(dst, bank[:], (ACT.Sigmoid, ACT.Tanh)[kind], scale=-1.0)
 
-        product(0, 0, gate0[:])
-        product(0, 1, gates[:, 0, :])
-        product(1, 0, cands[:, 0, :])
-        product(1, 1, cands[:, 1, :])
-        product(0, 2, gates[:, 1, :])
-        product(0, 3, gates[:, 2, :])
+        product(GATE, 0, gate0[:])
+        product(GATE, 1, gates[:, 0, :])
+        product(CAND, 0, cands[:, 0, :])
+        product(CAND, 1, cands[:, 1, :])
+        product(GATE, 2, gates[:, 1, :])
+        product(GATE, 3, gates[:, 2, :])
 
         rounded = keep.tile([P, U, PACK], BF16, name="rounded", align_bytes=64)
         o_codes = keep.tile([P, U], I32, name="o_codes", align_bytes=64)
         o_scales = keep.tile([P, U], U8, name="o_scales", align_bytes=64)
         kept, fresh = {}, {}
 
-        def look_up(t, dst):
-            kept[t] = dst
-            nc.vector.tensor_tensor(dst, win[t][:].indirect(slot_t[:]), act[0, t], ALU.mult)
+        def look_up(t):
+            nc.vector.tensor_tensor(kept[t][:], win[t][:].indirect(slot_t[:]), act[GATE, t], ALU.mult)
 
         def blend(t):
             fresh[t] = keep.tile([P, S], F32, name="fresh%d" % t)
-            nc.vector.scalar_tensor_tensor(fresh[t][:], act[0, t], 1.0, act[1, t], ALU.subtract, ALU.mult)
+            nc.vector.scalar_tensor_tensor(fresh[t][:], act[GATE, t], 1.0, act[CAND, t], ALU.subtract, ALU.mult)
 
         def put(t):
-            nc.vector.tensor_tensor(win[t][:].indirect(slot_t[:]), kept[t], fresh[t][:], ALU.add)
+            nc.vector.tensor_tensor(win[t][:].indirect(slot_t[:]), kept[t][:], fresh[t][:], ALU.add)
             nc.sync.dma_start(out_rows[:, t, :], win[t][:])
             if t != ORDER[-1]:
                 nc.scalar.copy(rounded[:, :, t], win[t][:])
 
-        for n in range(PACK):
-            kept[ORDER[n]] = keep.tile([P, S], F32, name="kept%d" % n, tag="kept%d" % n) if n else None
-        first = keep.tile([P, S], F32, name="first", tag="first")
-        look_up(ORDER[0], first[:])
-        look_up(ORDER[1], kept[ORDER[1]][:])
+        for n in range(1, PACK):
+            kept[ORDER[n]] = keep.tile([P, S], F32, name="kept%d" % n, tag="kept%d" % n)
+        kept[ORDER[0]] = keep.tile([P, S], F32, name="first", tag="first")
+
+        look_up(ORDER[0])
+        look_up(ORDER[1])
         blend(ORDER[0])
         blend(ORDER[1])
         put(ORDER[0])
         late = keep.tile([P, 2, S], F32, name="late", tag="first")
-        product(1, 2, late[:, 0, :])
-        product(1, 3, late[:, 1, :])
-        look_up(ORDER[2], kept[ORDER[2]][:])
-        look_up(ORDER[3], kept[ORDER[3]][:])
+        product(CAND, 2, late[:, 0, :])
+        product(CAND, 3, late[:, 1, :])
+        look_up(ORDER[2])
+        look_up(ORDER[3])
         put(ORDER[1])
         blend(ORDER[2])
         blend(ORDER[3])
         put(ORDER[2])
         put(ORDER[3])
-        t = ORDER[-1]
-        flat = rounded[:].rearrange("p u t -> p (u t)")
+
+        last = ORDER[-1]
+        values = rounded[:].rearrange("p u t -> p (u t)")
         words_out = out_1[0].rearrange("p c r -> p (c r)").bitcast(I32)
-        for c in (0, 2, 1, 3):
-            cols = slice(c * TAIL, (c + 1) * TAIL)
-            if c < 2:
-                nc.vector.tensor_copy(rounded[:, cols, t], win[t][:, cols])
-            else:
-                nc.scalar.copy(rounded[:, cols, t], win[t][:, cols])
-        for c in range(4):
-            cols = slice(c * TAIL, (c + 1) * TAIL)
-            nc.vector.quantize_mx(o_codes[:, cols].bitcast(FP8X4), o_scales[:, cols], flat[:, c * TAIL * 4 : (c + 1) * TAIL * 4])
+        for c in range(2):
+            mine = slice(c * CHUNK, (c + 1) * CHUNK)
+            other = slice((c + 2) * CHUNK, (c + 3) * CHUNK)
+            nc.vector.tensor_copy(rounded[:, mine, last], win[last][:, mine])
+            nc.scalar.copy(rounded[:, other, last], win[last][:, other])
+        stored = 0
+        for c in range(U // CHUNK):
+            cols = slice(c * CHUNK, (c + 1) * CHUNK)
+            nc.vector.quantize_mx(o_codes[:, cols].bitcast(FP8X4), o_scales[:, cols], values[:, PACK * cols.start : PACK * cols.stop])
             if c != 1:
-                done = slice(TAIL if c == 2 else c * TAIL, (c + 1) * TAIL)
-                nc.sync.dma_start(words_out[:, done], o_codes[:, done])
-        for q in range(4):
-            eng = nc.scalar if q else nc.sync
-            eng.dma_start(out_2[0, 4 * q : 4 * q + 4, :].bitcast(I32), o_scales[32 * q : 32 * q + 4, :].bitcast(I32))
+                nc.sync.dma_start(words_out[:, stored : cols.stop], o_codes[:, stored : cols.stop])
+                stored = cols.stop
+        for q in range(QUADS):
+            queue = nc.scalar if q else nc.sync
+            queue.dma_start(out_2[0, 4 * q : 4 * q + 4, :].bitcast(I32), o_scales[32 * q : 32 * q + 4, :].bitcast(I32))

@@ -46,7 +46,6 @@ def tile_picked_gmem_tanh_po_kernel(tc, x_words, x_scales, mem, w1, w2, offs, sl
 
         nc.sync.dma_start(xw[:], x_words[0].rearrange("p c r -> p (c r)").bitcast(I32))
         nc.sync.dma_start(offs_t[:], offs)
-        nc.sync.dma_start(slot_t[:], slot)
         for q in range(QUADS):
             queue = nc.scalar if q % 2 else nc.sync
             queue.dma_start(xs[32 * q : 32 * q + 4, :].bitcast(I32), x_scales[0, 4 * q : 4 * q + 4, :].bitcast(I32))
@@ -61,6 +60,8 @@ def tile_picked_gmem_tanh_po_kernel(tc, x_words, x_scales, mem, w1, w2, offs, sl
         for t in ORDER:
             win[t] = keep.tile([P, U], F32, name="win%d" % t, tag="win%d" % t)
             nc.sync.dma_start(win[t][:], mem_rows[:, t, :])
+            if t == ORDER[0]:
+                nc.sync.dma_start(slot_t[:], slot)
 
         xs_g = keep.tile([P, S], U8, name="xs_g", align_bytes=64)
         xw_g = keep.tile([P, S], U32, name="xw_g", align_bytes=64)

@@ -20,13 +20,13 @@ PACK = 4
 QUADS = 4
 GATE, CAND = 0, 1
 
-ORDER = (0, 2, 3, 1)
-
+ORDER = (0, 1, 2, 3)
 LOW, HIGH = slice(0, 2), slice(2, 4)
 W2_LOW_CUT = 40
 W2_HIGH_CUT = 64
-W1_HIGH_CUT = 72
-
+W1_LOW_CUT = 40
+W1_HIGH_CUT = 32
+PIECE = 256
 CHUNK = 256
 
 
@@ -68,7 +68,7 @@ def tile_picked_gmem_tanh_po_kernel(tc, x_words, x_scales, mem, w1, w2, offs, sl
         nc.vector.tensor_copy(xw_g[:], xw[:].bitcast(U32).indirect(offs_t[:]))
         nc.vector.tensor_copy(xs_g[:], xs[:].indirect(offs_t[:]))
 
-        def quantise(raw, name, on_scalar, on_vector, runs):
+        def regroup(raw, name, on_scalar, on_vector):
             grouped = keep.tile([P, PACK, P, PACK], BF16, name="grouped" + name, align_bytes=64)
             dst = grouped[:].rearrange("p t m j -> p m j t")
             src = raw[:].rearrange("p j (m t) -> p m j t", t=PACK)
@@ -79,36 +79,39 @@ def tile_picked_gmem_tanh_po_kernel(tc, x_words, x_scales, mem, w1, w2, offs, sl
             codes = keep.tile([P, N], U32, name="codes" + name, align_bytes=64)
             scales = keep.tile([P, N], U8, name="scales" + name, align_bytes=64)
             values = grouped[:].rearrange("p t m j -> p (t m j)")
-            for t0, t1 in runs:
-                cols = slice(t0 * P, t1 * P)
-                nc.vector.quantize_mx(codes[:, cols].bitcast(FP8X4), scales[:, cols], values[:, t0 * P * PACK : t1 * P * PACK])
-            return codes, scales
+            return codes, scales, values
 
-        weights = {
-            GATE: quantise(
-                raw2, "2",
-                ((slice(0, W2_LOW_CUT), LOW), (slice(0, W2_HIGH_CUT), HIGH)),
-                ((slice(W2_LOW_CUT, P), LOW), (slice(W2_HIGH_CUT, P), HIGH)),
-                ((0, 1), (1, 2), (2, 4)),
-            ),
-            CAND: quantise(
-                raw1, "1",
-                ((slice(0, W1_HIGH_CUT), HIGH),),
-                ((slice(0, P), LOW), (slice(W1_HIGH_CUT, P), HIGH)),
-                ((0, 2), (2, 4)),
-            ),
-        }
+        def pack(kind, t0, t1):
+            codes, scales, values = weights[kind]
+            cols = slice(t0 * P, t1 * P)
+            nc.vector.quantize_mx(codes[:, cols].bitcast(FP8X4), scales[:, cols], values[:, t0 * P * PACK : t1 * P * PACK])
+
+        weights = {}
+        weights[GATE] = regroup(
+            raw2, "2",
+            ((slice(0, W2_LOW_CUT), LOW), (slice(0, W2_HIGH_CUT), HIGH)),
+            ((slice(W2_LOW_CUT, P), LOW), (slice(W2_HIGH_CUT, P), HIGH)),
+        )
+        pack(GATE, 0, 1)
+        pack(GATE, 1, 2)
+        pack(GATE, 2, 4)
+        weights[CAND] = regroup(
+            raw1, "1",
+            ((slice(0, W1_LOW_CUT), LOW), (slice(0, W1_HIGH_CUT), HIGH)),
+            ((slice(W1_LOW_CUT, P), LOW), (slice(W1_HIGH_CUT, P), HIGH)),
+        )
+        pack(CAND, 0, 2)
 
         act = {}
         gate0 = keep.tile([P, S], F32, name="gate0")
         gates = keep.tile([P, PACK - 1, S], F32, name="gates", tag="raw1")
-        cands = keep.tile([P, 2, S], F32, name="cands")
+        cands = [keep.tile([P, S], F32, name="cand%d" % n, tag="cand%d" % n) for n in range(PACK)]
 
         def product(kind, n, dst):
             t = ORDER[n]
             cols = slice(t * P, (t + 1) * P)
-            codes, scales = weights[kind]
-            bank = psum.tile([P, S], F32, name="bank%d_%d" % (kind, t), tag="bank%d" % (n + 2 * kind))
+            codes, scales, values = weights[kind]
+            bank = psum.tile([P, S], F32, name="bank%d_%d" % (kind, t), tag="bank%d" % (PACK if (kind, n) == (GATE, 3) else n + PACK * kind))
             nc.tensor.matmul_mx(bank[:], lhsT=codes[:, cols].bitcast(FP8X4), lhsT_scale=scales[:, cols],
                                 rhs=xw_g[:].bitcast(FP8X4), rhs_scale=xs_g[:], start=True, stop=True)
             act[kind, t] = dst
@@ -116,62 +119,109 @@ def tile_picked_gmem_tanh_po_kernel(tc, x_words, x_scales, mem, w1, w2, offs, sl
 
         product(GATE, 0, gate0[:])
         product(GATE, 1, gates[:, 0, :])
-        product(CAND, 0, cands[:, 0, :])
-        product(CAND, 1, cands[:, 1, :])
+        product(CAND, 0, cands[0][:])
+        product(CAND, 1, cands[1][:])
         product(GATE, 2, gates[:, 1, :])
         product(GATE, 3, gates[:, 2, :])
 
-        rounded = keep.tile([P, U, PACK], BF16, name="rounded", align_bytes=64)
-        o_codes = keep.tile([P, U], I32, name="o_codes", align_bytes=64)
-        o_scales = keep.tile([P, U], U8, name="o_scales", align_bytes=64)
-        kept, fresh = {}, {}
+        kept, fresh, new = {}, {}, {}
 
         def look_up(t):
+            n = ORDER.index(t)
+            kept[t] = keep.tile([P, S], F32, name="kept%d" % t, tag="cand%d" % (n - 1) if n else "kept")
             nc.vector.tensor_tensor(kept[t][:], win[t][:].indirect(slot_t[:]), act[GATE, t], ALU.mult)
 
         def blend(t):
-            fresh[t] = keep.tile([P, S], F32, name="fresh%d" % t)
+            fresh[t] = keep.tile([P, S], F32, name="fresh%d" % t, tag="fresh%d" % t)
             nc.vector.scalar_tensor_tensor(fresh[t][:], act[GATE, t], 1.0, act[CAND, t], ALU.subtract, ALU.mult)
 
-        def put(t):
+        def put_by_scalar(t, pieces):
+            if t not in new:
+                new[t] = keep.tile([P, S], F32, name="new%d" % t, tag="new%d" % t)
+            span = slice(pieces[0] * PIECE, (pieces[-1] + 1) * PIECE)
+            nc.vector.tensor_tensor(new[t][:, span], kept[t][:, span], fresh[t][:, span], ALU.add)
+            return [(t, h) for h in pieces]
+
+        def scatter(t, h):
+            s = h * PIECE
+            nc.scalar.activation(win[t][:].indirect(slot_t[:, s // 16 : (s + PIECE) // 16]), new[t][:, s : s + PIECE], ACT.Copy)
+            if s + PIECE == S:
+                nc.sync.dma_start(out_rows[:, t, :], win[t][:])
+
+        def put_by_vector(t):
             nc.vector.tensor_tensor(win[t][:].indirect(slot_t[:]), kept[t][:], fresh[t][:], ALU.add)
             nc.sync.dma_start(out_rows[:, t, :], win[t][:])
-            if t != ORDER[-1]:
-                nc.scalar.copy(rounded[:, :, t], win[t][:])
 
-        for n in range(1, PACK):
-            kept[ORDER[n]] = keep.tile([P, S], F32, name="kept%d" % n, tag="kept%d" % n)
-        kept[ORDER[0]] = keep.tile([P, S], F32, name="first", tag="first")
 
-        look_up(ORDER[0])
-        look_up(ORDER[1])
-        blend(ORDER[0])
-        blend(ORDER[1])
-        put(ORDER[0])
-        late = keep.tile([P, 2, S], F32, name="late", tag="first")
-        product(CAND, 2, late[:, 0, :])
-        product(CAND, 3, late[:, 1, :])
-        look_up(ORDER[2])
-        look_up(ORDER[3])
-        put(ORDER[1])
-        blend(ORDER[2])
-        blend(ORDER[3])
-        put(ORDER[2])
-        put(ORDER[3])
+        a, b, c, d = ORDER
+        look_up(a)
+        blend(a)
+        pack(CAND, 2, 3)
+        product(CAND, 2, cands[2][:])
+        put_by_scalar(a, [0])
+        scatter(a, 0)
+        pack(CAND, 3, 4)
+        product(CAND, 3, cands[3][:])
+        look_up(b)
+        put_by_scalar(a, [1])
+        scatter(a, 1)
+        blend(b)
+        look_up(c)
+        put_by_scalar(b, [0])
+        scatter(b, 0)
+        blend(c)
+        look_up(d)
+        put_by_scalar(c, [0, 1])
+        scatter(c, 0)
+        put_by_scalar(b, [1])
+        scatter(b, 1)
+        scatter(c, 1)
+        blend(d)
+        spans = (slice(0, 512), slice(512, 768), slice(768, 1024))
+        pairs = {}
 
-        last = ORDER[-1]
-        values = rounded[:].rearrange("p u t -> p (u t)")
+        def round_phase(t, i, engine_copy):
+            if i not in pairs:
+                pairs[i] = keep.tile([P, 4 * (spans[i].stop - spans[i].start)], BF16, name="pairs%d" % i, tag=("raw1", "cand2", "fresh%d" % d)[i])
+            halves = pairs[i][:].rearrange("p (h u e) -> p h u e", h=2, e=2)
+            engine_copy(halves[:, t // 2, :, t % 2], win[t][:, spans[i]])
+
+        round_phase(a, 0, nc.vector.tensor_copy)
+        put_by_vector(d)
+        for i in (1, 2):
+            round_phase(a, i, nc.vector.tensor_copy)
+        for i in range(3):
+            round_phase(b, i, nc.vector.tensor_copy)
+        round_phase(d, 0, nc.vector.tensor_copy)
+        round_phase(c, 0, nc.vector.tensor_copy)
+        for i in (1, 2):
+            round_phase(d, i, nc.scalar.copy)
+            round_phase(c, i, nc.scalar.copy)
+
+        rounded = [keep.tile([P, CHUNK * PACK], BF16, name="rounded%d" % n, align_bytes=64) for n in range(U // CHUNK)]
+        o_codes = keep.tile([P, U], I32, name="o_codes", align_bytes=64)
+        o_scales = keep.tile([P, U], U8, name="o_scales", align_bytes=64)
         words_out = out_1[0].rearrange("p c r -> p (c r)").bitcast(I32)
-        for c in range(2):
-            mine = slice(c * CHUNK, (c + 1) * CHUNK)
-            other = slice((c + 2) * CHUNK, (c + 3) * CHUNK)
-            nc.vector.tensor_copy(rounded[:, mine, last], win[last][:, mine])
-            nc.scalar.copy(rounded[:, other, last], win[last][:, other])
+
+        def weave(n):
+            cols = slice(n * CHUNK, (n + 1) * CHUNK)
+            i = max(n - 1, 0)
+            woven = rounded[n][:].bitcast(U32).rearrange("p (u h) -> p u h", h=2)
+            source = pairs[i][:].bitcast(U32).rearrange("p (h u) -> p u h", h=2)
+            part = slice(cols.start - spans[i].start, cols.stop - spans[i].start)
+            if n == 3:
+                nc.scalar.copy(woven, source[:, part, :])
+            else:
+                nc.vector.tensor_copy(woven.bitcast(I32), source[:, part, :].bitcast(I32))
+
         stored = 0
-        for c in range(U // CHUNK):
-            cols = slice(c * CHUNK, (c + 1) * CHUNK)
-            nc.vector.quantize_mx(o_codes[:, cols].bitcast(FP8X4), o_scales[:, cols], values[:, PACK * cols.start : PACK * cols.stop])
-            if c != 1:
+        weave(0)
+        for n in range(U // CHUNK):
+            if n + 1 < U // CHUNK:
+                weave(n + 1)
+            cols = slice(n * CHUNK, (n + 1) * CHUNK)
+            nc.vector.quantize_mx(o_codes[:, cols].bitcast(FP8X4), o_scales[:, cols], rounded[n][:])
+            if n != 1:
                 nc.sync.dma_start(words_out[:, stored : cols.stop], o_codes[:, stored : cols.stop])
                 stored = cols.stop
         for q in range(QUADS):

@@ -19,13 +19,10 @@ P = 128
 PACK = 4
 QUADS = 4
 GATE, CAND = 0, 1
-
-ORDER = (0, 1, 2, 3)
-LOW, HIGH = slice(0, 2), slice(2, 4)
+LOW, HIGH = 0, 1
 W2_LOW_CUT = 40
-W2_HIGH_CUT = 64
-W1_LOW_CUT = 40
-W1_HIGH_CUT = 32
+W2_HIGH_CUT = 96
+W1_HIGH_CUT = 56
 PIECE = 256
 CHUNK = 256
 
@@ -50,165 +47,138 @@ def tile_picked_gmem_tanh_po_kernel(tc, x_words, x_scales, mem, w1, w2, offs, sl
             queue = nc.scalar if q % 2 else nc.sync
             queue.dma_start(xs[32 * q : 32 * q + 4, :].bitcast(I32), x_scales[0, 4 * q : 4 * q + 4, :].bitcast(I32))
         nc.scalar.activation(warm[:, 1:2], warm[:, 0:1], ACT.Sigmoid)
-        raw2 = keep.tile([P, PACK, N], F32, name="raw2")
-        nc.sync.dma_start(raw2[:], w2.rearrange("(p j) m -> p j m", j=PACK))
-        raw1 = keep.tile([P, PACK, N], F32, name="raw1", tag="raw1")
-        nc.sync.dma_start(raw1[:], w1.rearrange("(p j) m -> p j m", j=PACK))
         mem_rows = mem.rearrange("(p t) u -> p t u", t=PACK)
         out_rows = out_0.rearrange("(p t) u -> p t u", t=PACK)
-        win = {}
-        for t in ORDER:
-            win[t] = keep.tile([P, U], F32, name="win%d" % t, tag="win%d" % t)
+        raw = [keep.tile([P, PACK, N], F32, name="raw%d" % kind, tag="raw%d" % kind, align_bytes=64) for kind in (GATE, CAND)]
+        win = [keep.tile([P, U], F32, name="win%d" % t) for t in range(PACK)]
+        nc.sync.dma_start(raw[GATE][:], w2.rearrange("(p j) m -> p j m", j=PACK))
+        nc.sync.dma_start(raw[CAND][:], w1.rearrange("(p j) m -> p j m", j=PACK))
+        nc.sync.dma_start(win[0][:], mem_rows[:, 0, :])
+        nc.sync.dma_start(slot_t[:], slot)
+        for t in range(1, PACK):
             nc.sync.dma_start(win[t][:], mem_rows[:, t, :])
-            if t == ORDER[0]:
-                nc.sync.dma_start(slot_t[:], slot)
 
         xs_g = keep.tile([P, S], U8, name="xs_g", align_bytes=64)
         xw_g = keep.tile([P, S], U32, name="xw_g", align_bytes=64)
         nc.vector.tensor_copy(xw_g[:], xw[:].bitcast(U32).indirect(offs_t[:]))
         nc.vector.tensor_copy(xs_g[:], xs[:].indirect(offs_t[:]))
 
-        def regroup(raw, name, on_scalar, on_vector):
-            grouped = keep.tile([P, PACK, P, PACK], BF16, name="grouped" + name, align_bytes=64)
-            dst = grouped[:].rearrange("p t m j -> p m j t")
-            src = raw[:].rearrange("p j (m t) -> p m j t", t=PACK)
-            for groups, phases in on_scalar:
-                nc.scalar.copy(dst[:, groups, :, phases], src[:, groups, :, phases])
-            for groups, phases in on_vector:
-                nc.vector.tensor_copy(dst[:, groups, :, phases], src[:, groups, :, phases])
-            codes = keep.tile([P, N], U32, name="codes" + name, align_bytes=64)
-            scales = keep.tile([P, N], U8, name="scales" + name, align_bytes=64)
-            values = grouped[:].rearrange("p t m j -> p (t m j)")
-            return codes, scales, values
+        grouped, codes, scales = {}, {}, {}
+
+        def deal(copy, kind, first, last, half):
+            if (kind, half) not in grouped:
+                grouped[kind, half] = keep.tile([P, 2, P, PACK], BF16, name="grouped%d_%d" % (kind, half), align_bytes=64)
+            dst = grouped[kind, half][:].rearrange("p t m j -> p m j t")
+            src = raw[kind][:].rearrange("p j (m t) -> p m j t", t=PACK)
+            copy(dst[:, first:last], src[:, first:last, :, 2 * half : 2 * half + 2])
 
         def pack(kind, t0, t1):
-            codes, scales, values = weights[kind]
-            cols = slice(t0 * P, t1 * P)
-            nc.vector.quantize_mx(codes[:, cols].bitcast(FP8X4), scales[:, cols], values[:, t0 * P * PACK : t1 * P * PACK])
-
-        weights = {}
-        weights[GATE] = regroup(
-            raw2, "2",
-            ((slice(0, W2_LOW_CUT), LOW), (slice(0, W2_HIGH_CUT), HIGH)),
-            ((slice(W2_LOW_CUT, P), LOW), (slice(W2_HIGH_CUT, P), HIGH)),
-        )
-        pack(GATE, 0, 1)
-        pack(GATE, 1, 2)
-        pack(GATE, 2, 4)
-        weights[CAND] = regroup(
-            raw1, "1",
-            ((slice(0, W1_LOW_CUT), LOW), (slice(0, W1_HIGH_CUT), HIGH)),
-            ((slice(W1_LOW_CUT, P), LOW), (slice(W1_HIGH_CUT, P), HIGH)),
-        )
-        pack(CAND, 0, 2)
+            values = grouped[kind, t0 // 2][:].rearrange("p t m j -> p (t m j)")
+            key = kind, t0 // 2
+            if key not in codes:
+                codes[key] = keep.tile([P, 2 * P], U32, name="codes%d_%d" % key, tag="act0_0" if key == (CAND, HIGH) else "codes%d_%d" % key, align_bytes=64)
+                scales[key] = keep.tile([P, 2 * P], U8, name="scales%d_%d" % key, align_bytes=64)
+            cols = slice(t0 % 2 * P, (t0 % 2 + t1 - t0) * P)
+            nc.vector.quantize_mx(codes[key][:, cols].bitcast(FP8X4), scales[key][:, cols], values[:, cols.start * PACK : cols.stop * PACK])
 
         act = {}
-        gate0 = keep.tile([P, S], F32, name="gate0")
-        gates = keep.tile([P, PACK - 1, S], F32, name="gates", tag="raw1")
-        cands = [keep.tile([P, S], F32, name="cand%d" % n, tag="cand%d" % n) for n in range(PACK)]
 
-        def product(kind, n, dst):
-            t = ORDER[n]
-            cols = slice(t * P, (t + 1) * P)
-            codes, scales, values = weights[kind]
-            bank = psum.tile([P, S], F32, name="bank%d_%d" % (kind, t), tag="bank%d" % (PACK if (kind, n) == (GATE, 3) else n + PACK * kind))
-            nc.tensor.matmul_mx(bank[:], lhsT=codes[:, cols].bitcast(FP8X4), lhsT_scale=scales[:, cols],
+        def product(kind, t):
+            cols = slice(t % 2 * P, (t % 2 + 1) * P)
+            bank = psum.tile([P, S], F32, name="bank%d_%d" % (kind, t), tag="bank%d" % (PACK if (kind, t) == (GATE, 3) else t + PACK * kind))
+            nc.tensor.matmul_mx(bank[:], lhsT=codes[kind, t // 2][:, cols].bitcast(FP8X4), lhsT_scale=scales[kind, t // 2][:, cols],
                                 rhs=xw_g[:].bitcast(FP8X4), rhs_scale=xs_g[:], start=True, stop=True)
-            act[kind, t] = dst
-            nc.scalar.activation(dst, bank[:], (ACT.Sigmoid, ACT.Tanh)[kind], scale=-1.0)
-
-        product(GATE, 0, gate0[:])
-        product(GATE, 1, gates[:, 0, :])
-        product(CAND, 0, cands[0][:])
-        product(CAND, 1, cands[1][:])
-        product(GATE, 2, gates[:, 1, :])
-        product(GATE, 3, gates[:, 2, :])
+            act[kind, t] = keep.tile([P, S], F32, name="act%d_%d" % (kind, t), tag="act%d_%d" % (kind, t), align_bytes=64)
+            nc.scalar.activation(act[kind, t][:], bank[:], (ACT.Sigmoid, ACT.Tanh)[kind], scale=-1.0)
 
         kept, fresh, new = {}, {}, {}
 
         def look_up(t):
-            n = ORDER.index(t)
-            kept[t] = keep.tile([P, S], F32, name="kept%d" % t, tag="cand%d" % (n - 1) if n else "kept")
-            nc.vector.tensor_tensor(kept[t][:], win[t][:].indirect(slot_t[:]), act[GATE, t], ALU.mult)
+            kept[t] = keep.tile([P, S], F32, name="kept%d" % t, tag="act1_0" if t == 1 else "kept%d" % t, align_bytes=64)
+            nc.vector.tensor_tensor(kept[t][:], win[t][:].indirect(slot_t[:]), act[GATE, t][:], ALU.mult)
 
-        def blend(t):
-            fresh[t] = keep.tile([P, S], F32, name="fresh%d" % t, tag="fresh%d" % t)
-            nc.vector.scalar_tensor_tensor(fresh[t][:], act[GATE, t], 1.0, act[CAND, t], ALU.subtract, ALU.mult)
+        def blend(t, first, last):
+            if t not in fresh:
+                fresh[t] = keep.tile([P, S], F32, name="fresh%d" % t, tag="fresh%d" % t, align_bytes=64)
+            nc.vector.scalar_tensor_tensor(fresh[t][:, first:last], act[GATE, t][:, first:last], 1.0, act[CAND, t][:, first:last], ALU.subtract, ALU.mult)
 
-        def put_by_scalar(t, pieces):
-            if t not in new:
-                new[t] = keep.tile([P, S], F32, name="new%d" % t, tag="new%d" % t)
-            span = slice(pieces[0] * PIECE, (pieces[-1] + 1) * PIECE)
-            nc.vector.tensor_tensor(new[t][:, span], kept[t][:, span], fresh[t][:, span], ALU.add)
-            return [(t, h) for h in pieces]
+        def total(t, h):
+            span = slice(h * PIECE, (h + 1) * PIECE)
+            new[t, h] = keep.tile([P, PIECE], F32, name="new%d_%d" % (t, h), align_bytes=64)
+            nc.vector.tensor_tensor(new[t, h][:], kept[t][:, span], fresh[t][:, span], ALU.add)
 
         def scatter(t, h):
-            s = h * PIECE
-            nc.scalar.activation(win[t][:].indirect(slot_t[:, s // 16 : (s + PIECE) // 16]), new[t][:, s : s + PIECE], ACT.Copy)
-            if s + PIECE == S:
+            nc.scalar.activation(win[t][:].indirect(slot_t[:, h * PIECE // 16 : (h + 1) * PIECE // 16]), new[t, h][:], ACT.Copy)
+            if h == 1:
                 nc.sync.dma_start(out_rows[:, t, :], win[t][:])
 
-        def put_by_vector(t):
-            nc.vector.tensor_tensor(win[t][:].indirect(slot_t[:]), kept[t][:], fresh[t][:], ALU.add)
-            nc.sync.dma_start(out_rows[:, t, :], win[t][:])
+        deal(nc.scalar.copy, GATE, 0, W2_LOW_CUT, LOW)
+        deal(nc.vector.tensor_copy, GATE, W2_LOW_CUT, P, LOW)
+        deal(nc.scalar.copy, GATE, 0, W2_HIGH_CUT, HIGH)
+        pack(GATE, 0, 1)
+        deal(nc.vector.tensor_copy, GATE, W2_HIGH_CUT, P, HIGH)
+        pack(GATE, 1, 2)
+        pack(GATE, 2, 4)
+        for t in range(3):
+            product(GATE, t)
+        deal(nc.vector.tensor_copy, CAND, 0, P, LOW)
+        deal(nc.scalar.copy, CAND, 0, W1_HIGH_CUT, HIGH)
+        deal(nc.vector.tensor_copy, CAND, W1_HIGH_CUT, P, HIGH)
+        pack(CAND, 0, 1)
+        pack(CAND, 1, 2)
+        product(CAND, 0)
+        product(CAND, 1)
+        product(GATE, 3)
+        look_up(0)
+        blend(0, 0, PIECE)
+        blend(0, PIECE, S)
+        total(0, 0)
+        scatter(0, 0)
+        pack(CAND, 2, 4)
+        product(CAND, 2)
+        product(CAND, 3)
+        look_up(1)
+        blend(1, 0, S)
+        total(0, 1)
+        scatter(0, 1)
+        total(1, 0)
+        scatter(1, 0)
+        look_up(2)
+        blend(2, 0, S)
+        look_up(3)
+        total(2, 0)
+        scatter(2, 0)
+        total(1, 1)
+        scatter(1, 1)
+        blend(3, 0, S)
+        total(2, 1)
+        scatter(2, 1)
+        nc.vector.tensor_tensor(win[3][:].indirect(slot_t[:]), kept[3][:], fresh[3][:], ALU.add)
+        nc.sync.dma_start(out_rows[:, 3, :], win[3][:])
 
-
-        a, b, c, d = ORDER
-        look_up(a)
-        blend(a)
-        pack(CAND, 2, 3)
-        product(CAND, 2, cands[2][:])
-        put_by_scalar(a, [0])
-        scatter(a, 0)
-        pack(CAND, 3, 4)
-        product(CAND, 3, cands[3][:])
-        look_up(b)
-        put_by_scalar(a, [1])
-        scatter(a, 1)
-        blend(b)
-        look_up(c)
-        put_by_scalar(b, [0])
-        scatter(b, 0)
-        blend(c)
-        look_up(d)
-        put_by_scalar(c, [0, 1])
-        scatter(c, 0)
-        put_by_scalar(b, [1])
-        scatter(b, 1)
-        scatter(c, 1)
-        blend(d)
         spans = (slice(0, 512), slice(512, 768), slice(768, 1024))
-        pairs = {}
+        pairs = [keep.tile([P, 4 * (s.stop - s.start)], BF16, name="pairs%d" % i, tag=("act0_3", "fresh3", "kept3")[i], align_bytes=64) for i, s in enumerate(spans)]
 
-        def round_phase(t, i, engine_copy):
-            if i not in pairs:
-                pairs[i] = keep.tile([P, 4 * (spans[i].stop - spans[i].start)], BF16, name="pairs%d" % i, tag=("raw1", "cand2", "fresh%d" % d)[i])
+        def round_phase(t, i, copy):
             halves = pairs[i][:].rearrange("p (h u e) -> p h u e", h=2, e=2)
-            engine_copy(halves[:, t // 2, :, t % 2], win[t][:, spans[i]])
+            copy(halves[:, t // 2, :, t % 2], win[t][:, spans[i]])
 
-        round_phase(a, 0, nc.vector.tensor_copy)
-        put_by_vector(d)
-        for i in (1, 2):
-            round_phase(a, i, nc.vector.tensor_copy)
-        for i in range(3):
-            round_phase(b, i, nc.vector.tensor_copy)
-        round_phase(d, 0, nc.vector.tensor_copy)
-        round_phase(c, 0, nc.vector.tensor_copy)
-        for i in (1, 2):
-            round_phase(d, i, nc.scalar.copy)
-            round_phase(c, i, nc.scalar.copy)
+        for t, i in ((0, 0), (1, 0), (3, 0), (0, 1), (2, 0), (1, 1)):
+            round_phase(t, i, nc.vector.tensor_copy)
+        for t, i in ((0, 2), (3, 1), (2, 1), (1, 2), (3, 2), (2, 2)):
+            round_phase(t, i, nc.scalar.copy)
 
-        rounded = [keep.tile([P, CHUNK * PACK], BF16, name="rounded%d" % n, align_bytes=64) for n in range(U // CHUNK)]
+        rounded = {}
         o_codes = keep.tile([P, U], I32, name="o_codes", align_bytes=64)
         o_scales = keep.tile([P, U], U8, name="o_scales", align_bytes=64)
         words_out = out_1[0].rearrange("p c r -> p (c r)").bitcast(I32)
 
         def weave(n):
-            cols = slice(n * CHUNK, (n + 1) * CHUNK)
             i = max(n - 1, 0)
+            rounded[n] = keep.tile([P, CHUNK * PACK], BF16, name="rounded%d" % n, align_bytes=64)
             woven = rounded[n][:].bitcast(U32).rearrange("p (u h) -> p u h", h=2)
             source = pairs[i][:].bitcast(U32).rearrange("p (h u) -> p u h", h=2)
-            part = slice(cols.start - spans[i].start, cols.stop - spans[i].start)
+            part = slice(n * CHUNK - spans[i].start, (n + 1) * CHUNK - spans[i].start)
             if n == 3:
                 nc.scalar.copy(woven, source[:, part, :])
             else:

@@ -163,9 +163,9 @@ def tile_picked_gmem_tanh_po_kernel(tc, x_words, x_scales, mem, w1, w2, offs, sl
             halves = pairs[i][:].rearrange("p (h u e) -> p h u e", h=2, e=2)
             copy(halves[:, t // 2, :, t % 2], win[t][:, spans[i]])
 
-        for t, i in ((0, 0), (1, 0), (3, 0), (0, 1), (2, 0), (1, 1)):
+        for t, i in ((0, 0), (1, 0), (3, 0), (0, 1), (0, 2), (1, 2), (2, 0), (1, 1)):
             round_phase(t, i, nc.vector.tensor_copy)
-        for t, i in ((0, 2), (3, 1), (2, 1), (1, 2), (3, 2), (2, 2)):
+        for t, i in ((3, 2), (2, 2), (3, 1), (2, 1)):
             round_phase(t, i, nc.scalar.copy)
 
         rounded = {}

@@ -22,7 +22,8 @@ GATE, CAND = 0, 1
 LOW, HIGH = 0, 1
 W2_LOW_CUT = 40
 W2_HIGH_CUT = 96
-W1_HIGH_CUT = 56
+W1_HIGH_CUT = 64
+BANK = ((0, 1, 2, 3), (2, 3, 4, 5))
 PIECE = 256
 CHUNK = 256
 
@@ -85,7 +86,7 @@ def tile_picked_gmem_tanh_po_kernel(tc, x_words, x_scales, mem, w1, w2, offs, sl
 
         def product(kind, t):
             cols = slice(t % 2 * P, (t % 2 + 1) * P)
-            bank = psum.tile([P, S], F32, name="bank%d_%d" % (kind, t), tag="bank%d" % (PACK if (kind, t) == (GATE, 3) else t + PACK * kind))
+            bank = psum.tile([P, S], F32, name="bank%d_%d" % (kind, t), tag="bank%d" % BANK[kind][t])
             nc.tensor.matmul_mx(bank[:], lhsT=codes[kind, t // 2][:, cols].bitcast(FP8X4), lhsT_scale=scales[kind, t // 2][:, cols],
                                 rhs=xw_g[:].bitcast(FP8X4), rhs_scale=xs_g[:], start=True, stop=True)
             act[kind, t] = keep.tile([P, S], F32, name="act%d_%d" % (kind, t), tag="act%d_%d" % (kind, t), align_bytes=64)
@@ -119,7 +120,7 @@ def tile_picked_gmem_tanh_po_kernel(tc, x_words, x_scales, mem, w1, w2, offs, sl
         deal(nc.vector.tensor_copy, GATE, W2_HIGH_CUT, P, HIGH)
         pack(GATE, 1, 2)
         pack(GATE, 2, 4)
-        for t in range(3):
+        for t in range(2):
             product(GATE, t)
         deal(nc.vector.tensor_copy, CAND, 0, P, LOW)
         deal(nc.scalar.copy, CAND, 0, W1_HIGH_CUT, HIGH)
@@ -128,12 +129,13 @@ def tile_picked_gmem_tanh_po_kernel(tc, x_words, x_scales, mem, w1, w2, offs, sl
         pack(CAND, 1, 2)
         product(CAND, 0)
         product(CAND, 1)
-        product(GATE, 3)
+        product(GATE, 2)
         look_up(0)
         blend(0, 0, PIECE)
         blend(0, PIECE, S)
         total(0, 0)
         scatter(0, 0)
+        product(GATE, 3)
         pack(CAND, 2, 4)
         product(CAND, 2)
         product(CAND, 3)

@@ -22,8 +22,9 @@ GATE, CAND = 0, 1
 LOW, HIGH = 0, 1
 W2_LOW_CUT = 40
 W2_HIGH_CUT = 96
-W1_HIGH_CUT = 64
-BANK = ((0, 1, 2, 3), (2, 3, 4, 5))
+W1_HIGH_CUT = 32
+BANK = ((0, 1, 2, 3), (3, 4, 5, 6))
+SPARE_BANK = 7
 PIECE = 256
 CHUNK = 256
 
@@ -84,13 +85,14 @@ def tile_picked_gmem_tanh_po_kernel(tc, x_words, x_scales, mem, w1, w2, offs, sl
 
         act = {}
 
-        def product(kind, t):
+        def product(kind, t, first=0, last=S):
             cols = slice(t % 2 * P, (t % 2 + 1) * P)
-            bank = psum.tile([P, S], F32, name="bank%d_%d" % (kind, t), tag="bank%d" % BANK[kind][t])
+            bank = psum.tile([P, last - first], F32, name="bank%d_%d_%d" % (kind, t, first), tag="bank%d" % (SPARE_BANK if first else BANK[kind][t]))
             nc.tensor.matmul_mx(bank[:], lhsT=codes[kind, t // 2][:, cols].bitcast(FP8X4), lhsT_scale=scales[kind, t // 2][:, cols],
-                                rhs=xw_g[:].bitcast(FP8X4), rhs_scale=xs_g[:], start=True, stop=True)
-            act[kind, t] = keep.tile([P, S], F32, name="act%d_%d" % (kind, t), tag="act%d_%d" % (kind, t), align_bytes=64)
-            nc.scalar.activation(act[kind, t][:], bank[:], (ACT.Sigmoid, ACT.Tanh)[kind], scale=-1.0)
+                                rhs=xw_g[:, first:last].bitcast(FP8X4), rhs_scale=xs_g[:, first:last], start=True, stop=True)
+            if (kind, t) not in act:
+                act[kind, t] = keep.tile([P, S], F32, name="act%d_%d" % (kind, t), tag="act%d_%d" % (kind, t), align_bytes=64)
+            nc.scalar.activation(act[kind, t][:, first:last], bank[:], (ACT.Sigmoid, ACT.Tanh)[kind], scale=-1.0)
 
         kept, fresh, new = {}, {}, {}
 
@@ -120,8 +122,10 @@ def tile_picked_gmem_tanh_po_kernel(tc, x_words, x_scales, mem, w1, w2, offs, sl
         deal(nc.vector.tensor_copy, GATE, W2_HIGH_CUT, P, HIGH)
         pack(GATE, 1, 2)
         pack(GATE, 2, 4)
-        for t in range(2):
-            product(GATE, t)
+        product(GATE, 0, 0, PIECE)
+        product(GATE, 0, PIECE, S)
+        product(GATE, 1)
+        product(GATE, 2)
         deal(nc.vector.tensor_copy, CAND, 0, P, LOW)
         deal(nc.scalar.copy, CAND, 0, W1_HIGH_CUT, HIGH)
         deal(nc.vector.tensor_copy, CAND, W1_HIGH_CUT, P, HIGH)
@@ -129,13 +133,12 @@ def tile_picked_gmem_tanh_po_kernel(tc, x_words, x_scales, mem, w1, w2, offs, sl
         pack(CAND, 1, 2)
         product(CAND, 0)
         product(CAND, 1)
-        product(GATE, 2)
+        product(GATE, 3)
         look_up(0)
         blend(0, 0, PIECE)
         blend(0, PIECE, S)
         total(0, 0)
         scatter(0, 0)
-        product(GATE, 3)
         pack(CAND, 2, 4)
         product(CAND, 2)
         product(CAND, 3)
@@ -186,16 +189,22 @@ def tile_picked_gmem_tanh_po_kernel(tc, x_words, x_scales, mem, w1, w2, offs, sl
             else:
                 nc.vector.tensor_copy(woven.bitcast(I32), source[:, part, :].bitcast(I32))
 
-        stored = 0
+        def pack_result(n, first, last):
+            cols = slice(n * CHUNK + first, n * CHUNK + last)
+            nc.vector.quantize_mx(o_codes[:, cols].bitcast(FP8X4), o_scales[:, cols], rounded[n][:, first * PACK : last * PACK])
+
         weave(0)
-        for n in range(U // CHUNK):
-            if n + 1 < U // CHUNK:
-                weave(n + 1)
-            cols = slice(n * CHUNK, (n + 1) * CHUNK)
-            nc.vector.quantize_mx(o_codes[:, cols].bitcast(FP8X4), o_scales[:, cols], rounded[n][:])
-            if n != 1:
-                nc.sync.dma_start(words_out[:, stored : cols.stop], o_codes[:, stored : cols.stop])
-                stored = cols.stop
+        weave(1)
+        pack_result(0, 0, CHUNK)
+        weave(2)
+        pack_result(1, 0, CHUNK // 2)
+        nc.sync.dma_start(words_out[:, 0:384], o_codes[:, 0:384])
+        pack_result(1, CHUNK // 2, CHUNK)
+        weave(3)
+        pack_result(2, 0, CHUNK)
+        nc.sync.dma_start(words_out[:, 384:768], o_codes[:, 384:768])
+        pack_result(3, 0, CHUNK)
+        nc.sync.dma_start(words_out[:, 768:U], o_codes[:, 768:U])
         for q in range(QUADS):
             queue = nc.scalar if q else nc.sync
             queue.dma_start(out_2[0, 4 * q : 4 * q + 4, :].bitcast(I32), o_scales[32 * q : 32 * q + 4, :].bitcast(I32))

@@ -1,6 +1,7 @@
 from contextlib import ExitStack
 
 import concourse.mybir as mybir
+from concourse.masks import make_identity
 
 K, T, S, N, U = 512, 1024, 512, 512, 1024
 FLOPS = 2 * 2 * K * N * S
@@ -22,11 +23,10 @@ GATE, CAND = 0, 1
 LOW, HIGH = 0, 1
 W2_LOW_CUT = 40
 W2_HIGH_CUT = 96
-W1_HIGH_CUT = 32
+W1_HIGH_CUT = 48
 BANK = ((0, 1, 2, 3), (3, 4, 5, 6))
-SPARE_BANK = 7
+SPARE_BANK = (7, 0)
 PIECE = 256
-CHUNK = 256
 
 
 def tile_picked_gmem_tanh_po_kernel(tc, x_words, x_scales, mem, w1, w2, offs, slot, out_0, out_1, out_2):
@@ -42,6 +42,8 @@ def tile_picked_gmem_tanh_po_kernel(tc, x_words, x_scales, mem, w1, w2, offs, sl
         nc.vector.memset(xs[:].bitcast(I32), 0)
         warm = keep.tile([P, 2], F32, name="warm")
         nc.vector.memset(warm[:, 0:1], 0.0)
+        one = keep.tile([P, 1], F32, name="one")
+        nc.vector.memset(one[:], 1.0)
 
         nc.sync.dma_start(xw[:], x_words[0].rearrange("p c r -> p (c r)").bitcast(I32))
         nc.sync.dma_start(offs_t[:], offs)
@@ -49,6 +51,8 @@ def tile_picked_gmem_tanh_po_kernel(tc, x_words, x_scales, mem, w1, w2, offs, sl
             queue = nc.scalar if q % 2 else nc.sync
             queue.dma_start(xs[32 * q : 32 * q + 4, :].bitcast(I32), x_scales[0, 4 * q : 4 * q + 4, :].bitcast(I32))
         nc.scalar.activation(warm[:, 1:2], warm[:, 0:1], ACT.Sigmoid)
+        ident = keep.tile([P, P], F32, name="ident")
+        make_identity(nc, ident[:])
         mem_rows = mem.rearrange("(p t) u -> p t u", t=PACK)
         out_rows = out_0.rearrange("(p t) u -> p t u", t=PACK)
         raw = [keep.tile([P, PACK, N], F32, name="raw%d" % kind, tag="raw%d" % kind, align_bytes=64) for kind in (GATE, CAND)]
@@ -87,7 +91,7 @@ def tile_picked_gmem_tanh_po_kernel(tc, x_words, x_scales, mem, w1, w2, offs, sl
 
         def product(kind, t, first=0, last=S):
             cols = slice(t % 2 * P, (t % 2 + 1) * P)
-            bank = psum.tile([P, last - first], F32, name="bank%d_%d_%d" % (kind, t, first), tag="bank%d" % (SPARE_BANK if first else BANK[kind][t]))
+            bank = psum.tile([P, last - first], F32, name="bank%d_%d_%d" % (kind, t, first), tag="bank%d" % (SPARE_BANK[kind] if first else BANK[kind][t]))
             nc.tensor.matmul_mx(bank[:], lhsT=codes[kind, t // 2][:, cols].bitcast(FP8X4), lhsT_scale=scales[kind, t // 2][:, cols],
                                 rhs=xw_g[:, first:last].bitcast(FP8X4), rhs_scale=xs_g[:, first:last], start=True, stop=True)
             if (kind, t) not in act:
@@ -105,14 +109,13 @@ def tile_picked_gmem_tanh_po_kernel(tc, x_words, x_scales, mem, w1, w2, offs, sl
                 fresh[t] = keep.tile([P, S], F32, name="fresh%d" % t, tag="fresh%d" % t, align_bytes=64)
             nc.vector.scalar_tensor_tensor(fresh[t][:, first:last], act[GATE, t][:, first:last], 1.0, act[CAND, t][:, first:last], ALU.subtract, ALU.mult)
 
-        def total(t, h):
-            span = slice(h * PIECE, (h + 1) * PIECE)
-            new[t, h] = keep.tile([P, PIECE], F32, name="new%d_%d" % (t, h), align_bytes=64)
-            nc.vector.tensor_tensor(new[t, h][:], kept[t][:, span], fresh[t][:, span], ALU.add)
+        def total(t, first, last):
+            new[t, first] = keep.tile([P, last - first], F32, name="new%d_%d" % (t, first), tag="new%d_%d" % (t, first), align_bytes=64)
+            nc.vector.tensor_tensor(new[t, first][:], kept[t][:, first:last], fresh[t][:, first:last], ALU.add)
 
-        def scatter(t, h):
-            nc.scalar.activation(win[t][:].indirect(slot_t[:, h * PIECE // 16 : (h + 1) * PIECE // 16]), new[t, h][:], ACT.Copy)
-            if h == 1:
+        def scatter(t, first, last):
+            nc.scalar.activation(win[t][:].indirect(slot_t[:, first // 16 : last // 16]), new[t, first][:], ACT.Copy, scale=one[:])
+            if last == S:
                 nc.sync.dma_start(out_rows[:, t, :], win[t][:])
 
         deal(nc.scalar.copy, GATE, 0, W2_LOW_CUT, LOW)
@@ -131,80 +134,75 @@ def tile_picked_gmem_tanh_po_kernel(tc, x_words, x_scales, mem, w1, w2, offs, sl
         deal(nc.vector.tensor_copy, CAND, W1_HIGH_CUT, P, HIGH)
         pack(CAND, 0, 1)
         pack(CAND, 1, 2)
-        product(CAND, 0)
+        product(CAND, 0, 0, PIECE)
+        product(CAND, 0, PIECE, S)
         product(CAND, 1)
         product(GATE, 3)
         look_up(0)
         blend(0, 0, PIECE)
         blend(0, PIECE, S)
-        total(0, 0)
-        scatter(0, 0)
+        total(0, 0, PIECE)
+        scatter(0, 0, PIECE)
         pack(CAND, 2, 4)
         product(CAND, 2)
         product(CAND, 3)
         look_up(1)
         blend(1, 0, S)
-        total(0, 1)
-        scatter(0, 1)
-        total(1, 0)
-        scatter(1, 0)
+        total(0, PIECE, S)
+        scatter(0, PIECE, S)
+        total(1, 0, S)
+        scatter(1, 0, S)
         look_up(2)
         blend(2, 0, S)
         look_up(3)
-        total(2, 0)
-        scatter(2, 0)
-        total(1, 1)
-        scatter(1, 1)
         blend(3, 0, S)
-        total(2, 1)
-        scatter(2, 1)
+        total(2, 0, S)
+        scatter(2, 0, S)
         nc.vector.tensor_tensor(win[3][:].indirect(slot_t[:]), kept[3][:], fresh[3][:], ALU.add)
         nc.sync.dma_start(out_rows[:, 3, :], win[3][:])
 
-        spans = (slice(0, 512), slice(512, 768), slice(768, 1024))
-        pairs = [keep.tile([P, 4 * (s.stop - s.start)], BF16, name="pairs%d" % i, tag=("act0_3", "fresh3", "kept3")[i], align_bytes=64) for i, s in enumerate(spans)]
-
-        def round_phase(t, i, copy):
-            halves = pairs[i][:].rearrange("p (h u e) -> p h u e", h=2, e=2)
-            copy(halves[:, t // 2, :, t % 2], win[t][:, spans[i]])
-
-        for t, i in ((0, 0), (1, 0), (3, 0), (0, 1), (0, 2), (1, 2), (2, 0), (1, 1)):
-            round_phase(t, i, nc.vector.tensor_copy)
-        for t, i in ((3, 2), (2, 2), (3, 1), (2, 1)):
-            round_phase(t, i, nc.scalar.copy)
-
-        rounded = {}
         o_codes = keep.tile([P, U], I32, name="o_codes", align_bytes=64)
         o_scales = keep.tile([P, U], U8, name="o_scales", align_bytes=64)
         words_out = out_1[0].rearrange("p c r -> p (c r)").bitcast(I32)
+        spans = (slice(0, 384), slice(384, 640), slice(640, 896), slice(896, U))
+        rounded = [keep.tile([P, PACK * (s.stop - s.start)], BF16, name="rounded%d" % i, align_bytes=64) for i, s in enumerate(spans)]
 
-        def weave(n):
-            i = max(n - 1, 0)
-            rounded[n] = keep.tile([P, CHUNK * PACK], BF16, name="rounded%d" % n, align_bytes=64)
-            woven = rounded[n][:].bitcast(U32).rearrange("p (u h) -> p u h", h=2)
-            source = pairs[i][:].bitcast(U32).rearrange("p (h u) -> p u h", h=2)
-            part = slice(n * CHUNK - spans[i].start, (n + 1) * CHUNK - spans[i].start)
-            if n == 3:
-                nc.scalar.copy(woven, source[:, part, :])
-            else:
-                nc.vector.tensor_copy(woven.bitcast(I32), source[:, part, :].bitcast(I32))
+        blocks = [slice(spans[2].start + b * P, spans[2].start + (b + 1) * P) for b in range(3)]
+        both = psum.tile([P, 2, 2, P], F32, name="both", tag="bank0")
+        turned = {(0, 0): both[:, 0], (0, 1): both[:, 1]}
+        for n, key in enumerate(((0, 2), (1, 0), (1, 1), (1, 2))):
+            turned[key] = psum.tile([P, 2, P], F32, name="turned%d_%d" % key, tag="bank%d" % (1 + n))[:]
+        for t in (0, 1, 3, 2):
+            for b in range(3):
+                nc.tensor.transpose(turned[t // 2, b][:, t % 2, :], win[t][:, blocks[b]], ident[:])
+        rows_both = keep.tile([P, 2, P, 2], BF16, name="rows_both", tag="new2_0", align_bytes=64)
+        nc.scalar.copy(rows_both[:], both[:].rearrange("u b e p -> u b p e"))
+        words_both = rows_both[:].rearrange("u b p e -> u (b p e)").bitcast(F32)
+        words = {(0, 0): words_both[:, 0:P], (0, 1): words_both[:, P : 2 * P]}
+        for key in ((0, 2), (1, 0), (1, 1), (1, 2)):
+            rows = keep.tile([P, P, 2], BF16, name="rows%d_%d" % key, tag="fresh2" if key == (0, 2) else "rows%d_%d" % key, align_bytes=64)
+            nc.scalar.copy(rows[:], turned[key].rearrange("u e p -> u p e"))
+            words[key] = rows[:].rearrange("u p e -> u (p e)").bitcast(F32)
+        back = [psum.tile([P, 2, P], F32, name="back%d" % b, tag="bank%d" % (5 + b)) for b in range(3)]
+        for h in range(2):
+            for b in range(3):
+                nc.tensor.transpose(back[b][:, h, :], words[h, b], ident[:])
+        for b in range(3):
+            woven = rounded[2 + b // 2][:].bitcast(F32)[:, b % 2 * 2 * P : (b % 2 + 1) * 2 * P]
+            nc.scalar.copy(woven.rearrange("p (u h) -> p u h", h=2), back[b][:].rearrange("p h u -> p u h"))
 
-        def pack_result(n, first, last):
-            cols = slice(n * CHUNK + first, n * CHUNK + last)
-            nc.vector.quantize_mx(o_codes[:, cols].bitcast(FP8X4), o_scales[:, cols], rounded[n][:, first * PACK : last * PACK])
-
-        weave(0)
-        weave(1)
-        pack_result(0, 0, CHUNK)
-        weave(2)
-        pack_result(1, 0, CHUNK // 2)
-        nc.sync.dma_start(words_out[:, 0:384], o_codes[:, 0:384])
-        pack_result(1, CHUNK // 2, CHUNK)
-        weave(3)
-        pack_result(2, 0, CHUNK)
-        nc.sync.dma_start(words_out[:, 384:768], o_codes[:, 384:768])
-        pack_result(3, 0, CHUNK)
-        nc.sync.dma_start(words_out[:, 768:U], o_codes[:, 768:U])
+        pairs = [keep.tile([P, PACK * (spans[i].stop - spans[i].start)], BF16, name="pairs%d" % i, tag=("fresh3", "kept3")[i], align_bytes=64) for i in range(2)]
+        for t, i in ((0, 0), (1, 0), (3, 0), (0, 1), (1, 1), (3, 1), (2, 0), (2, 1)):
+            halves = pairs[i][:].rearrange("p (h u e) -> p h u e", h=2, e=2)
+            nc.vector.tensor_copy(halves[:, t // 2, :, t % 2], win[t][:, spans[i]])
+        for i in range(2):
+            woven = rounded[i][:].bitcast(I32).rearrange("p (u h) -> p u h", h=2)
+            nc.vector.tensor_copy(woven, pairs[i][:].bitcast(I32).rearrange("p (h u) -> p u h", h=2))
+        stores = {0: slice(0, 384), 1: slice(384, 640), 3: slice(640, U)}
+        for i, s in enumerate(spans):
+            nc.vector.quantize_mx(o_codes[:, s].bitcast(FP8X4), o_scales[:, s], rounded[i][:])
+            if i in stores:
+                nc.sync.dma_start(words_out[:, stores[i]], o_codes[:, stores[i]])
         for q in range(QUADS):
             queue = nc.scalar if q else nc.sync
             queue.dma_start(out_2[0, 4 * q : 4 * q + 4, :].bitcast(I32), o_scales[32 * q : 32 * q + 4, :].bitcast(I32))

@@ -1,7 +1,6 @@
 from contextlib import ExitStack
 
 import concourse.mybir as mybir
-from concourse.masks import make_identity
 
 K, T, S, N, U = 512, 1024, 512, 512, 1024
 FLOPS = 2 * 2 * K * N * S
@@ -42,8 +41,6 @@ def tile_picked_gmem_tanh_po_kernel(tc, x_words, x_scales, mem, w1, w2, offs, sl
         nc.vector.memset(xs[:].bitcast(I32), 0)
         warm = keep.tile([P, 2], F32, name="warm")
         nc.vector.memset(warm[:, 0:1], 0.0)
-        one = keep.tile([P, 1], F32, name="one")
-        nc.vector.memset(one[:], 1.0)
 
         nc.sync.dma_start(xw[:], x_words[0].rearrange("p c r -> p (c r)").bitcast(I32))
         nc.sync.dma_start(offs_t[:], offs)
@@ -52,7 +49,15 @@ def tile_picked_gmem_tanh_po_kernel(tc, x_words, x_scales, mem, w1, w2, offs, sl
             queue.dma_start(xs[32 * q : 32 * q + 4, :].bitcast(I32), x_scales[0, 4 * q : 4 * q + 4, :].bitcast(I32))
         nc.scalar.activation(warm[:, 1:2], warm[:, 0:1], ACT.Sigmoid)
         ident = keep.tile([P, P], F32, name="ident")
-        make_identity(nc, ident[:])
+        ones = keep.tile([P, P], F32, name="ones")
+        column = keep.tile([P, P], F32, name="column", align_bytes=64)
+        row = keep.tile([P, 32], F32, name="row", align_bytes=64)
+        nc.vector.memset(ones[:], 1.0)
+        nc.vector.tensor_tensor_scan(column[:], ones[:], ones[:], 0.0, ALU.mult, ALU.add)
+        nc.vector.transpose(row[:], column[:, 0:32])
+        for q in range(QUADS):
+            rows = slice(32 * q, 32 * q + 32)
+            nc.vector.tensor_scalar(ident[rows, :], column[rows, :], row[rows, 0:1], 32.0 * q, ALU.subtract, ALU.is_equal)
         mem_rows = mem.rearrange("(p t) u -> p t u", t=PACK)
         out_rows = out_0.rearrange("(p t) u -> p t u", t=PACK)
         raw = [keep.tile([P, PACK, N], F32, name="raw%d" % kind, tag="raw%d" % kind, align_bytes=64) for kind in (GATE, CAND)]
@@ -114,7 +119,7 @@ def tile_picked_gmem_tanh_po_kernel(tc, x_words, x_scales, mem, w1, w2, offs, sl
             nc.vector.tensor_tensor(new[t, first][:], kept[t][:, first:last], fresh[t][:, first:last], ALU.add)
 
         def scatter(t, first, last):
-            nc.scalar.activation(win[t][:].indirect(slot_t[:, first // 16 : last // 16]), new[t, first][:], ACT.Copy, scale=one[:])
+            nc.scalar.activation(win[t][:].indirect(slot_t[:, first // 16 : last // 16]), new[t, first][:], ACT.Copy, scale=ones[:, 0:1])
             if last == S:
                 nc.sync.dma_start(out_rows[:, t, :], win[t][:])
 

@@ -169,7 +169,7 @@ def tile_picked_gmem_tanh_po_kernel(tc, x_words, x_scales, mem, w1, w2, offs, sl
         o_codes = keep.tile([P, U], I32, name="o_codes", align_bytes=64)
         o_scales = keep.tile([P, U], U8, name="o_scales", align_bytes=64)
         words_out = out_1[0].rearrange("p c r -> p (c r)").bitcast(I32)
-        spans = (slice(0, 384), slice(384, 640), slice(640, 896), slice(896, U))
+        spans = (slice(0, 384), slice(768, U), slice(384, 640), slice(640, 768))
         rounded = [keep.tile([P, PACK * (s.stop - s.start)], BF16, name="rounded%d" % i, align_bytes=64) for i, s in enumerate(spans)]
 
         blocks = [slice(spans[2].start + b * P, spans[2].start + (b + 1) * P) for b in range(3)]
@@ -197,17 +197,30 @@ def tile_picked_gmem_tanh_po_kernel(tc, x_words, x_scales, mem, w1, w2, offs, sl
             nc.scalar.copy(woven.rearrange("p (u h) -> p u h", h=2), back[b][:].rearrange("p h u -> p u h"))
 
         pairs = [keep.tile([P, PACK * (spans[i].stop - spans[i].start)], BF16, name="pairs%d" % i, tag=("fresh3", "kept3")[i], align_bytes=64) for i in range(2)]
-        for t, i in ((0, 0), (1, 0), (3, 0), (0, 1), (1, 1), (3, 1), (2, 0), (2, 1)):
+
+        def round_phase(t, i):
             halves = pairs[i][:].rearrange("p (h u e) -> p h u e", h=2, e=2)
             nc.vector.tensor_copy(halves[:, t // 2, :, t % 2], win[t][:, spans[i]])
-        for i in range(2):
+
+        def weave(i):
             woven = rounded[i][:].bitcast(I32).rearrange("p (u h) -> p u h", h=2)
             nc.vector.tensor_copy(woven, pairs[i][:].bitcast(I32).rearrange("p (h u) -> p u h", h=2))
-        stores = {0: slice(0, 384), 1: slice(384, 640), 3: slice(640, U)}
-        for i, s in enumerate(spans):
-            nc.vector.quantize_mx(o_codes[:, s].bitcast(FP8X4), o_scales[:, s], rounded[i][:])
-            if i in stores:
-                nc.sync.dma_start(words_out[:, stores[i]], o_codes[:, stores[i]])
+
+        def pack_result(i):
+            nc.vector.quantize_mx(o_codes[:, spans[i]].bitcast(FP8X4), o_scales[:, spans[i]], rounded[i][:])
+
+        for t, i in ((0, 0), (1, 0), (3, 0), (0, 1), (1, 1), (2, 0), (3, 1)):
+            round_phase(t, i)
+        weave(0)
+        round_phase(2, 1)
+        pack_result(0)
+        nc.sync.dma_start(words_out[:, 0:384], o_codes[:, 0:384])
+        weave(1)
+        pack_result(2)
+        pack_result(3)
+        nc.sync.dma_start(words_out[:, 384:768], o_codes[:, 384:768])
+        pack_result(1)
+        nc.sync.dma_start(words_out[:, 768:U], o_codes[:, 768:U])
         for q in range(QUADS):
-            queue = nc.scalar if q else nc.sync
+            queue = nc.scalar if q >= 2 else nc.sync
             queue.dma_start(out_2[0, 4 * q : 4 * q + 4, :].bitcast(I32), o_scales[32 * q : 32 * q + 4, :].bitcast(I32))

@@ -32,6 +32,7 @@ def tile_picked_gmem_tanh_po_kernel(tc, x_words, x_scales, mem, w1, w2, offs, sl
     nc = tc.nc
     with ExitStack() as ctx:
         keep = ctx.enter_context(tc.tile_pool(name="keep", bufs=1))
+        shared = ctx.enter_context(tc.tile_pool(name="shared", bufs=1))
         psum = ctx.enter_context(tc.psum_pool(name="psum", bufs=1))
 
         offs_t = keep.tile([P, S // 16], U16, name="offs_t")
@@ -78,7 +79,10 @@ def tile_picked_gmem_tanh_po_kernel(tc, x_words, x_scales, mem, w1, w2, offs, sl
 
         def deal(copy, kind, first, last, half):
             if (kind, half) not in grouped:
-                grouped[kind, half] = keep.tile([P, 2, P, PACK], BF16, name="grouped%d_%d" % (kind, half), align_bytes=64)
+                if (kind, half) == (CAND, HIGH):
+                    grouped[kind, half] = shared.tile([P, 2, P, PACK], BF16, name="late_weights", offset=1024, align_bytes=64)
+                else:
+                    grouped[kind, half] = keep.tile([P, 2, P, PACK], BF16, name="grouped%d_%d" % (kind, half), align_bytes=64)
             dst = grouped[kind, half][:].rearrange("p t m j -> p m j t")
             src = raw[kind][:].rearrange("p j (m t) -> p m j t", t=PACK)
             copy(dst[:, first:last], src[:, first:last, :, 2 * half : 2 * half + 2])
@@ -103,20 +107,48 @@ def tile_picked_gmem_tanh_po_kernel(tc, x_words, x_scales, mem, w1, w2, offs, sl
                 act[kind, t] = keep.tile([P, S], F32, name="act%d_%d" % (kind, t), tag="act%d_%d" % (kind, t), align_bytes=64)
             nc.scalar.activation(act[kind, t][:, first:last], bank[:], (ACT.Sigmoid, ACT.Tanh)[kind], scale=-1.0)
 
+        def turned_products(kind_cols, banks, targets):
+            width = kind_cols.stop - kind_cols.start
+            key = CAND, min(targets) // 2
+            per_bank = S // width
+            for t, tag in targets.items():
+                act[CAND, t] = psum.tile([P, S], F32, name="cand%d" % t, tag=tag)
+            for n, tag in enumerate(banks):
+                bank = psum.tile([P, S], F32, name="across%d_%d" % (min(targets), n), tag=tag)
+                for g in range(per_bank):
+                    picked = slice((n * per_bank + g) * P, (n * per_bank + g + 1) * P)
+                    nc.tensor.matmul_mx(bank[:, g * width : (g + 1) * width], lhsT=xw_g[:, picked].bitcast(FP8X4), lhsT_scale=xs_g[:, picked],
+                                        rhs=codes[key][:, kind_cols].bitcast(FP8X4), rhs_scale=scales[key][:, kind_cols], start=True, stop=True)
+                across = keep.tile([P, S], F32, name="tanh%d_%d" % (min(targets), n), align_bytes=64)
+                nc.scalar.activation(across[:], bank[:], ACT.Tanh, scale=-1.0)
+                for i, t in enumerate(sorted(targets)):
+                    for g in range(per_bank):
+                        picked = slice((n * per_bank + g) * P, (n * per_bank + g + 1) * P)
+                        nc.tensor.transpose(act[CAND, t][:, picked], across[:, g * width + i * P : g * width + (i + 1) * P], ident[:])
+
         kept, fresh, new = {}, {}, {}
 
-        def look_up(t):
-            kept[t] = keep.tile([P, S], F32, name="kept%d" % t, tag="act1_0" if t == 1 else "kept%d" % t, align_bytes=64)
-            nc.vector.tensor_tensor(kept[t][:], win[t][:].indirect(slot_t[:]), act[GATE, t][:], ALU.mult)
+        def look_up(t, first=0, last=S):
+            if first == 0:
+                kept[t] = keep.tile([P, S], F32, name="kept%d" % t, tag=("kept0", "act1_0", "act0_1", "act1_0")[t], align_bytes=64)
+            nc.vector.tensor_tensor(kept[t][:, first:last], win[t][:].indirect(slot_t[:, first // 16 : last // 16]), act[GATE, t][:, first:last], ALU.mult)
 
         def blend(t, first, last):
-            if t not in fresh:
-                fresh[t] = keep.tile([P, S], F32, name="fresh%d" % t, tag="fresh%d" % t, align_bytes=64)
-            nc.vector.scalar_tensor_tensor(fresh[t][:, first:last], act[GATE, t][:, first:last], 1.0, act[CAND, t][:, first:last], ALU.subtract, ALU.mult)
+            if last < S:
+                fresh[t, first] = shared.tile([P, last - first], F32, name="first_fresh", offset=0, align_bytes=64)
+            else:
+                fresh[t, first] = keep.tile([P, last - first], F32, name="fresh%d" % t, tag="fresh%d" % t, align_bytes=64)
+            nc.vector.scalar_tensor_tensor(fresh[t, first][:], act[GATE, t][:, first:last], 1.0, act[CAND, t][:, first:last], ALU.subtract, ALU.mult)
 
-        def total(t, first, last):
-            new[t, first] = keep.tile([P, last - first], F32, name="new%d_%d" % (t, first), tag="new%d_%d" % (t, first), align_bytes=64)
-            nc.vector.tensor_tensor(new[t, first][:], kept[t][:, first:last], fresh[t][:, first:last], ALU.add)
+        def total(t, first, last, aside=0):
+            if first:
+                new[t, first] = shared.tile([P, last - first], F32, name="late_new", offset=512, align_bytes=64)
+            else:
+                new[t, first] = keep.tile([P, last - first], F32, name="new%d_0" % t, tag="new%d_0" % t, align_bytes=64)
+            if aside:
+                nc.gpsimd.tensor_tensor(new[t, first][:, 0:aside], kept[t][:, first : first + aside], fresh[t, first][:, 0:aside], ALU.add)
+            if first + aside < last:
+                nc.vector.tensor_tensor(new[t, first][:, aside:], kept[t][:, first + aside : last], fresh[t, first][:, aside:], ALU.add)
 
         def scatter(t, first, last):
             nc.scalar.activation(win[t][:].indirect(slot_t[:, first // 16 : last // 16]), new[t, first][:], ACT.Copy, scale=ones[:, 0:1])
@@ -141,7 +173,7 @@ def tile_picked_gmem_tanh_po_kernel(tc, x_words, x_scales, mem, w1, w2, offs, sl
         pack(CAND, 1, 2)
         product(CAND, 0, 0, PIECE)
         product(CAND, 0, PIECE, S)
-        product(CAND, 1)
+        turned_products(slice(P, 2 * P), ("bank4",), {1: "bank1"})
         product(GATE, 3)
         look_up(0)
         blend(0, 0, PIECE)
@@ -149,21 +181,21 @@ def tile_picked_gmem_tanh_po_kernel(tc, x_words, x_scales, mem, w1, w2, offs, sl
         total(0, 0, PIECE)
         scatter(0, 0, PIECE)
         pack(CAND, 2, 4)
-        product(CAND, 2)
-        product(CAND, 3)
+        turned_products(slice(0, 2 * P), ("bank5", "bank6"), {2: "bank2", 3: "bank7"})
         look_up(1)
         blend(1, 0, S)
-        total(0, PIECE, S)
+        total(0, PIECE, S, PIECE)
         scatter(0, PIECE, S)
+        look_up(2)
         total(1, 0, S)
         scatter(1, 0, S)
-        look_up(2)
+        look_up(3, 0, PIECE)
         blend(2, 0, S)
-        look_up(3)
+        look_up(3, PIECE, S)
         blend(3, 0, S)
-        total(2, 0, S)
+        total(2, 0, S, PIECE)
         scatter(2, 0, S)
-        nc.vector.tensor_tensor(win[3][:].indirect(slot_t[:]), kept[3][:], fresh[3][:], ALU.add)
+        nc.vector.tensor_tensor(win[3][:].indirect(slot_t[:]), kept[3][:], fresh[3, 0][:], ALU.add)
         nc.sync.dma_start(out_rows[:, 3, :], win[3][:])
 
         o_codes = keep.tile([P, U], I32, name="o_codes", align_bytes=64)
@@ -196,7 +228,7 @@ def tile_picked_gmem_tanh_po_kernel(tc, x_words, x_scales, mem, w1, w2, offs, sl
             woven = rounded[2 + b // 2][:].bitcast(F32)[:, b % 2 * 2 * P : (b % 2 + 1) * 2 * P]
             nc.scalar.copy(woven.rearrange("p (u h) -> p u h", h=2), back[b][:].rearrange("p h u -> p u h"))
 
-        pairs = [keep.tile([P, PACK * (spans[i].stop - spans[i].start)], BF16, name="pairs%d" % i, tag=("fresh3", "kept3")[i], align_bytes=64) for i in range(2)]
+        pairs = [keep.tile([P, PACK * (spans[i].stop - spans[i].start)], BF16, name="pairs%d" % i, tag=("fresh3", "act1_0")[i], align_bytes=64) for i in range(2)]
 
         def round_phase(t, i):
             halves = pairs[i][:].rearrange("p (h u e) -> p h u e", h=2, e=2)

@@ -22,7 +22,7 @@ GATE, CAND = 0, 1
 LOW, HIGH = 0, 1
 W2_LOW_CUT = 40
 W2_HIGH_CUT = 96
-W1_HIGH_CUT = 48
+W1_HIGH_CUT = 32
 BANK = ((0, 1, 2, 3), (3, 4, 5, 6))
 SPARE_BANK = (7, 0)
 PIECE = 256
@@ -130,7 +130,7 @@ def tile_picked_gmem_tanh_po_kernel(tc, x_words, x_scales, mem, w1, w2, offs, sl
 
         def look_up(t, first=0, last=S):
             if first == 0:
-                kept[t] = keep.tile([P, S], F32, name="kept%d" % t, tag=("kept0", "act1_0", "act0_1", "act1_0")[t], align_bytes=64)
+                kept[t] = keep.tile([P, S], F32, name="kept%d" % t, tag="act1_0" if t == 1 else "kept%d" % t, align_bytes=64)
             nc.vector.tensor_tensor(kept[t][:, first:last], win[t][:].indirect(slot_t[:, first // 16 : last // 16]), act[GATE, t][:, first:last], ALU.mult)
 
         def blend(t, first, last):
@@ -181,17 +181,17 @@ def tile_picked_gmem_tanh_po_kernel(tc, x_words, x_scales, mem, w1, w2, offs, sl
         total(0, 0, PIECE)
         scatter(0, 0, PIECE)
         pack(CAND, 2, 4)
-        turned_products(slice(0, 2 * P), ("bank5", "bank6"), {2: "bank2", 3: "bank7"})
+        turned_products(slice(0, P), ("bank5",), {2: "bank2"})
+        turned_products(slice(P, 2 * P), ("bank6",), {3: "bank7"})
         look_up(1)
         blend(1, 0, S)
         total(0, PIECE, S, PIECE)
         scatter(0, PIECE, S)
         look_up(2)
-        total(1, 0, S)
+        total(1, 0, S, PIECE)
         scatter(1, 0, S)
-        look_up(3, 0, PIECE)
         blend(2, 0, S)
-        look_up(3, PIECE, S)
+        look_up(3)
         blend(3, 0, S)
         total(2, 0, S, PIECE)
         scatter(2, 0, S)
@@ -228,7 +228,7 @@ def tile_picked_gmem_tanh_po_kernel(tc, x_words, x_scales, mem, w1, w2, offs, sl
             woven = rounded[2 + b // 2][:].bitcast(F32)[:, b % 2 * 2 * P : (b % 2 + 1) * 2 * P]
             nc.scalar.copy(woven.rearrange("p (u h) -> p u h", h=2), back[b][:].rearrange("p h u -> p u h"))
 
-        pairs = [keep.tile([P, PACK * (spans[i].stop - spans[i].start)], BF16, name="pairs%d" % i, tag=("fresh3", "act1_0")[i], align_bytes=64) for i in range(2)]
+        pairs = [keep.tile([P, PACK * (spans[i].stop - spans[i].start)], BF16, name="pairs%d" % i, tag=("fresh3", "kept3")[i], align_bytes=64) for i in range(2)]
 
         def round_phase(t, i):
             halves = pairs[i][:].rearrange("p (h u e) -> p h u e", h=2, e=2)
@@ -241,18 +241,16 @@ def tile_picked_gmem_tanh_po_kernel(tc, x_words, x_scales, mem, w1, w2, offs, sl
         def pack_result(i):
             nc.vector.quantize_mx(o_codes[:, spans[i]].bitcast(FP8X4), o_scales[:, spans[i]], rounded[i][:])
 
-        for t, i in ((0, 0), (1, 0), (3, 0), (0, 1), (1, 1), (2, 0), (3, 1)):
+        for t, i in ((0, 0), (1, 0), (3, 0), (0, 1), (1, 1), (3, 1), (2, 0), (2, 1)):
             round_phase(t, i)
-        weave(0)
-        round_phase(2, 1)
-        pack_result(0)
-        nc.sync.dma_start(words_out[:, 0:384], o_codes[:, 0:384])
-        weave(1)
+        for i in range(2):
+            weave(i)
+        for i in range(2):
+            pack_result(i)
+            nc.sync.dma_start(words_out[:, spans[i]], o_codes[:, spans[i]])
         pack_result(2)
         pack_result(3)
         nc.sync.dma_start(words_out[:, 384:768], o_codes[:, 384:768])
-        pack_result(1)
-        nc.sync.dma_start(words_out[:, 768:U], o_codes[:, 768:U])
         for q in range(QUADS):
             queue = nc.scalar if q >= 2 else nc.sync
             queue.dma_start(out_2[0, 4 * q : 4 * q + 4, :].bitcast(I32), o_scales[32 * q : 32 * q + 4, :].bitcast(I32))

from contextlib import ExitStack

import concourse.mybir as mybir

K, T, S, N, U = 512, 1024, 512, 512, 1024
FLOPS = 2 * 2 * K * N * S

F32 = mybir.dt.float32
BF16 = mybir.dt.bfloat16
I32 = mybir.dt.int32
U32 = mybir.dt.uint32
U16 = mybir.dt.uint16
U8 = mybir.dt.uint8
FP8X4 = mybir.dt.float8_e4m3fn_x4
ACT = mybir.ActivationFunctionType
ALU = mybir.AluOpType

P = 128
PACK = 4
QUADS = 4
GATE, CAND = 0, 1
LOW, HIGH = 0, 1
W2_LOW_CUT = 40
W2_HIGH_CUT = 96
W1_HIGH_CUT = 32
BANK = ((0, 1, 2, 3), (3, 4, 5, 6))
SPARE_BANK = (7, 0)
PIECE = 256


def tile_picked_gmem_tanh_po_kernel(tc, x_words, x_scales, mem, w1, w2, offs, slot, out_0, out_1, out_2):
    nc = tc.nc
    with ExitStack() as ctx:
        keep = ctx.enter_context(tc.tile_pool(name="keep", bufs=1))
        shared = ctx.enter_context(tc.tile_pool(name="shared", bufs=1))
        psum = ctx.enter_context(tc.psum_pool(name="psum", bufs=1))

        offs_t = keep.tile([P, S // 16], U16, name="offs_t")
        slot_t = keep.tile([P, S // 16], U16, name="slot_t")
        xw = keep.tile([P, T], I32, name="xw", align_bytes=64)
        xs = keep.tile([P, T], U8, name="xs", align_bytes=64)
        nc.vector.memset(xs[:].bitcast(I32), 0)
        warm = keep.tile([P, 2], F32, name="warm")
        nc.vector.memset(warm[:, 0:1], 0.0)

        nc.sync.dma_start(xw[:], x_words[0].rearrange("p c r -> p (c r)").bitcast(I32))
        nc.sync.dma_start(offs_t[:], offs)
        for q in range(QUADS):
            queue = nc.scalar if q % 2 else nc.sync
            queue.dma_start(xs[32 * q : 32 * q + 4, :].bitcast(I32), x_scales[0, 4 * q : 4 * q + 4, :].bitcast(I32))
        nc.scalar.activation(warm[:, 1:2], warm[:, 0:1], ACT.Sigmoid)
        ident = keep.tile([P, P], F32, name="ident")
        ones = keep.tile([P, P], F32, name="ones")
        column = keep.tile([P, P], F32, name="column", align_bytes=64)
        row = keep.tile([P, 32], F32, name="row", align_bytes=64)
        nc.vector.memset(ones[:], 1.0)
        nc.vector.tensor_tensor_scan(column[:], ones[:], ones[:], 0.0, ALU.mult, ALU.add)
        nc.vector.transpose(row[:], column[:, 0:32])
        for q in range(QUADS):
            rows = slice(32 * q, 32 * q + 32)
            nc.vector.tensor_scalar(ident[rows, :], column[rows, :], row[rows, 0:1], 32.0 * q, ALU.subtract, ALU.is_equal)
        mem_rows = mem.rearrange("(p t) u -> p t u", t=PACK)
        out_rows = out_0.rearrange("(p t) u -> p t u", t=PACK)
        raw = [keep.tile([P, PACK, N], F32, name="raw%d" % kind, tag="raw%d" % kind, align_bytes=64) for kind in (GATE, CAND)]
        win = [keep.tile([P, U], F32, name="win%d" % t) for t in range(PACK)]
        nc.sync.dma_start(raw[GATE][:], w2.rearrange("(p j) m -> p j m", j=PACK))
        nc.sync.dma_start(raw[CAND][:], w1.rearrange("(p j) m -> p j m", j=PACK))
        nc.sync.dma_start(win[0][:], mem_rows[:, 0, :])
        nc.sync.dma_start(slot_t[:], slot)
        for t in range(1, PACK):
            nc.sync.dma_start(win[t][:], mem_rows[:, t, :])

        xs_g = keep.tile([P, S], U8, name="xs_g", align_bytes=64)
        xw_g = keep.tile([P, S], U32, name="xw_g", align_bytes=64)
        nc.vector.tensor_copy(xw_g[:], xw[:].bitcast(U32).indirect(offs_t[:]))
        nc.vector.tensor_copy(xs_g[:], xs[:].indirect(offs_t[:]))

        grouped, codes, scales = {}, {}, {}

        def deal(copy, kind, first, last, half):
            if (kind, half) not in grouped:
                if (kind, half) == (CAND, HIGH):
                    grouped[kind, half] = shared.tile([P, 2, P, PACK], BF16, name="late_weights", offset=1024, align_bytes=64)
                else:
                    grouped[kind, half] = keep.tile([P, 2, P, PACK], BF16, name="grouped%d_%d" % (kind, half), align_bytes=64)
            dst = grouped[kind, half][:].rearrange("p t m j -> p m j t")
            src = raw[kind][:].rearrange("p j (m t) -> p m j t", t=PACK)
            copy(dst[:, first:last], src[:, first:last, :, 2 * half : 2 * half + 2])

        def pack(kind, t0, t1):
            values = grouped[kind, t0 // 2][:].rearrange("p t m j -> p (t m j)")
            key = kind, t0 // 2
            if key not in codes:
                codes[key] = keep.tile([P, 2 * P], U32, name="codes%d_%d" % key, tag="act0_0" if key == (CAND, HIGH) else "codes%d_%d" % key, align_bytes=64)
                scales[key] = keep.tile([P, 2 * P], U8, name="scales%d_%d" % key, align_bytes=64)
            cols = slice(t0 % 2 * P, (t0 % 2 + t1 - t0) * P)
            nc.vector.quantize_mx(codes[key][:, cols].bitcast(FP8X4), scales[key][:, cols], values[:, cols.start * PACK : cols.stop * PACK])

        act = {}

        def product(kind, t, first=0, last=S):
            cols = slice(t % 2 * P, (t % 2 + 1) * P)
            bank = psum.tile([P, last - first], F32, name="bank%d_%d_%d" % (kind, t, first), tag="bank%d" % (SPARE_BANK[kind] if first else BANK[kind][t]))
            nc.tensor.matmul_mx(bank[:], lhsT=codes[kind, t // 2][:, cols].bitcast(FP8X4), lhsT_scale=scales[kind, t // 2][:, cols],
                                rhs=xw_g[:, first:last].bitcast(FP8X4), rhs_scale=xs_g[:, first:last], start=True, stop=True)
            if (kind, t) not in act:
                act[kind, t] = keep.tile([P, S], F32, name="act%d_%d" % (kind, t), tag="act%d_%d" % (kind, t), align_bytes=64)
            nc.scalar.activation(act[kind, t][:, first:last], bank[:], (ACT.Sigmoid, ACT.Tanh)[kind], scale=-1.0)

        def turned_products(kind_cols, banks, targets):
            width = kind_cols.stop - kind_cols.start
            key = CAND, min(targets) // 2
            per_bank = S // width
            for t, tag in targets.items():
                act[CAND, t] = psum.tile([P, S], F32, name="cand%d" % t, tag=tag)
            for n, tag in enumerate(banks):
                bank = psum.tile([P, S], F32, name="across%d_%d" % (min(targets), n), tag=tag)
                for g in range(per_bank):
                    picked = slice((n * per_bank + g) * P, (n * per_bank + g + 1) * P)
                    nc.tensor.matmul_mx(bank[:, g * width : (g + 1) * width], lhsT=xw_g[:, picked].bitcast(FP8X4), lhsT_scale=xs_g[:, picked],
                                        rhs=codes[key][:, kind_cols].bitcast(FP8X4), rhs_scale=scales[key][:, kind_cols], start=True, stop=True)
                across = keep.tile([P, S], F32, name="tanh%d_%d" % (min(targets), n), align_bytes=64)
                nc.scalar.activation(across[:], bank[:], ACT.Tanh, scale=-1.0)
                for i, t in enumerate(sorted(targets)):
                    for g in range(per_bank):
                        picked = slice((n * per_bank + g) * P, (n * per_bank + g + 1) * P)
                        nc.tensor.transpose(act[CAND, t][:, picked], across[:, g * width + i * P : g * width + (i + 1) * P], ident[:])

        kept, fresh, new = {}, {}, {}

        def look_up(t, first=0, last=S):
            if first == 0:
                kept[t] = keep.tile([P, S], F32, name="kept%d" % t, tag="act1_0" if t == 1 else "kept%d" % t, align_bytes=64)
            nc.vector.tensor_tensor(kept[t][:, first:last], win[t][:].indirect(slot_t[:, first // 16 : last // 16]), act[GATE, t][:, first:last], ALU.mult)

        def blend(t, first, last):
            if last < S:
                fresh[t, first] = shared.tile([P, last - first], F32, name="first_fresh", offset=0, align_bytes=64)
            else:
                fresh[t, first] = keep.tile([P, last - first], F32, name="fresh%d" % t, tag="fresh%d" % t, align_bytes=64)
            nc.vector.scalar_tensor_tensor(fresh[t, first][:], act[GATE, t][:, first:last], 1.0, act[CAND, t][:, first:last], ALU.subtract, ALU.mult)

        def total(t, first, last, aside=0):
            if first:
                new[t, first] = shared.tile([P, last - first], F32, name="late_new", offset=512, align_bytes=64)
            else:
                new[t, first] = keep.tile([P, last - first], F32, name="new%d_0" % t, tag="new%d_0" % t, align_bytes=64)
            if aside:
                nc.gpsimd.tensor_tensor(new[t, first][:, 0:aside], kept[t][:, first : first + aside], fresh[t, first][:, 0:aside], ALU.add)
            if first + aside < last:
                nc.vector.tensor_tensor(new[t, first][:, aside:], kept[t][:, first + aside : last], fresh[t, first][:, aside:], ALU.add)

        def scatter(t, first, last):
            nc.scalar.activation(win[t][:].indirect(slot_t[:, first // 16 : last // 16]), new[t, first][:], ACT.Copy, scale=ones[:, 0:1])
            if last == S:
                nc.sync.dma_start(out_rows[:, t, :], win[t][:])

        deal(nc.scalar.copy, GATE, 0, W2_LOW_CUT, LOW)
        deal(nc.vector.tensor_copy, GATE, W2_LOW_CUT, P, LOW)
        deal(nc.scalar.copy, GATE, 0, W2_HIGH_CUT, HIGH)
        pack(GATE, 0, 1)
        deal(nc.vector.tensor_copy, GATE, W2_HIGH_CUT, P, HIGH)
        pack(GATE, 1, 2)
        pack(GATE, 2, 4)
        product(GATE, 0, 0, PIECE)
        product(GATE, 0, PIECE, S)
        product(GATE, 1)
        product(GATE, 2)
        deal(nc.vector.tensor_copy, CAND, 0, P, LOW)
        deal(nc.scalar.copy, CAND, 0, W1_HIGH_CUT, HIGH)
        deal(nc.vector.tensor_copy, CAND, W1_HIGH_CUT, P, HIGH)
        pack(CAND, 0, 1)
        pack(CAND, 1, 2)
        product(CAND, 0, 0, PIECE)
        product(CAND, 0, PIECE, S)
        turned_products(slice(P, 2 * P), ("bank4",), {1: "bank1"})
        product(GATE, 3)
        look_up(0)
        blend(0, 0, PIECE)
        blend(0, PIECE, S)
        total(0, 0, PIECE)
        scatter(0, 0, PIECE)
        pack(CAND, 2, 4)
        turned_products(slice(0, P), ("bank5",), {2: "bank2"})
        turned_products(slice(P, 2 * P), ("bank6",), {3: "bank7"})
        look_up(1)
        blend(1, 0, S)
        total(0, PIECE, S, PIECE)
        scatter(0, PIECE, S)
        look_up(2)
        total(1, 0, S, PIECE)
        scatter(1, 0, S)
        blend(2, 0, S)
        look_up(3)
        blend(3, 0, S)
        total(2, 0, S, PIECE)
        scatter(2, 0, S)
        nc.vector.tensor_tensor(win[3][:].indirect(slot_t[:]), kept[3][:], fresh[3, 0][:], ALU.add)
        nc.sync.dma_start(out_rows[:, 3, :], win[3][:])

        o_codes = keep.tile([P, U], I32, name="o_codes", align_bytes=64)
        o_scales = keep.tile([P, U], U8, name="o_scales", align_bytes=64)
        words_out = out_1[0].rearrange("p c r -> p (c r)").bitcast(I32)
        spans = (slice(0, 384), slice(768, U), slice(384, 640), slice(640, 768))
        rounded = [keep.tile([P, PACK * (s.stop - s.start)], BF16, name="rounded%d" % i, align_bytes=64) for i, s in enumerate(spans)]

        blocks = [slice(spans[2].start + b * P, spans[2].start + (b + 1) * P) for b in range(3)]
        both = psum.tile([P, 2, 2, P], F32, name="both", tag="bank0")
        turned = {(0, 0): both[:, 0], (0, 1): both[:, 1]}
        for n, key in enumerate(((0, 2), (1, 0), (1, 1), (1, 2))):
            turned[key] = psum.tile([P, 2, P], F32, name="turned%d_%d" % key, tag="bank%d" % (1 + n))[:]
        for t in (0, 1, 3, 2):
            for b in range(3):
                nc.tensor.transpose(turned[t // 2, b][:, t % 2, :], win[t][:, blocks[b]], ident[:])
        rows_both = keep.tile([P, 2, P, 2], BF16, name="rows_both", tag="new2_0", align_bytes=64)
        nc.scalar.copy(rows_both[:], both[:].rearrange("u b e p -> u b p e"))
        words_both = rows_both[:].rearrange("u b p e -> u (b p e)").bitcast(F32)
        words = {(0, 0): words_both[:, 0:P], (0, 1): words_both[:, P : 2 * P]}
        for key in ((0, 2), (1, 0), (1, 1), (1, 2)):
            rows = keep.tile([P, P, 2], BF16, name="rows%d_%d" % key, tag="fresh2" if key == (0, 2) else "rows%d_%d" % key, align_bytes=64)
            nc.scalar.copy(rows[:], turned[key].rearrange("u e p -> u p e"))
            words[key] = rows[:].rearrange("u p e -> u (p e)").bitcast(F32)
        back = [psum.tile([P, 2, P], F32, name="back%d" % b, tag="bank%d" % (5 + b)) for b in range(3)]
        for h in range(2):
            for b in range(3):
                nc.tensor.transpose(back[b][:, h, :], words[h, b], ident[:])
        for b in range(3):
            woven = rounded[2 + b // 2][:].bitcast(F32)[:, b % 2 * 2 * P : (b % 2 + 1) * 2 * P]
            nc.scalar.copy(woven.rearrange("p (u h) -> p u h", h=2), back[b][:].rearrange("p h u -> p u h"))

        pairs = [keep.tile([P, PACK * (spans[i].stop - spans[i].start)], BF16, name="pairs%d" % i, tag=("fresh3", "kept3")[i], align_bytes=64) for i in range(2)]

        def round_phase(t, i):
            halves = pairs[i][:].rearrange("p (h u e) -> p h u e", h=2, e=2)
            nc.vector.tensor_copy(halves[:, t // 2, :, t % 2], win[t][:, spans[i]])

        def weave(i):
            woven = rounded[i][:].bitcast(I32).rearrange("p (u h) -> p u h", h=2)
            nc.vector.tensor_copy(woven, pairs[i][:].bitcast(I32).rearrange("p (h u) -> p u h", h=2))

        def pack_result(i):
            nc.vector.quantize_mx(o_codes[:, spans[i]].bitcast(FP8X4), o_scales[:, spans[i]], rounded[i][:])

        for t, i in ((0, 0), (1, 0), (3, 0), (0, 1), (1, 1), (3, 1), (2, 0), (2, 1)):
            round_phase(t, i)
        for i in range(2):
            weave(i)
        for i in range(2):
            pack_result(i)
            nc.sync.dma_start(words_out[:, spans[i]], o_codes[:, spans[i]])
        pack_result(2)
        pack_result(3)
        nc.sync.dma_start(words_out[:, 384:768], o_codes[:, 384:768])
        for q in range(QUADS):
            queue = nc.scalar if q >= 2 else nc.sync
            queue.dma_start(out_2[0, 4 * q : 4 * q + 4, :].bitcast(I32), o_scales[32 * q : 32 * q + 4, :].bitcast(I32))
